import numpy as np
import ml_dtypes


def mxq(x, axis, fmt="e4m3"):
    dtype, down = {"e4m3": (ml_dtypes.float8_e4m3fn, 7), "e5m2": (ml_dtypes.float8_e5m2, 14)}[fmt]
    v = np.moveaxis(np.asarray(x, np.float32).astype(ml_dtypes.bfloat16).astype(np.float64), axis, -1)
    blocks = v.reshape(v.shape[:-1] + (-1, 32))
    amax = np.abs(blocks).max(-1, keepdims=True)
    byte = np.maximum(np.where(amax > 0, np.frexp(amax)[1] - 1 + 127, 0) - down, 1)
    scale = np.exp2(byte - 127.0)
    codes = (blocks / scale).astype(np.float32).astype(dtype).astype(np.float64)
    return np.moveaxis((codes * scale).reshape(v.shape), -1, axis)


WIDE = False


def mx_kscale(k):
    if not WIDE:
        return np.ones(k)
    levels = np.array([10, -10, 5, -5, 0])
    if k % 512:
        return np.exp2(np.random.permutation(np.resize(levels, k // 32))).repeat(32)
    a = np.empty((k // 512, 16))
    for p in range(k // 512):
        a[p, :8] = np.random.permutation(np.resize(levels, 8))
        for g in range(8):
            far = levels[np.abs(levels - a[p, g]) >= 10]
            a[p, g + 8] = far[np.random.randint(len(far))]
    return np.exp2(a.ravel()).repeat(32)


BF16 = ml_dtypes.bfloat16


def bf(x):
    return np.asarray(x, np.float32).astype(BF16)


def f64(x):
    return np.asarray(x).astype(np.float64)


E2M1 = np.array([0.0, 0.5, 1.0, 1.5, 2.0, 3.0, 4.0, 6.0, -0.0, -0.5, -1.0, -1.5, -2.0, -3.0, -4.0, -6.0])


def pack_weight(w, fmt):
    k, n = w.shape
    w = f64(bf(w)).reshape(k // 32, 32, n)
    amax = np.abs(w).max(1)
    if fmt == "e4m3":
        byte = np.frexp(amax)[1] - 1 + 127 - 7
    else:
        mant, ex = np.frexp(amax / 6.0)
        byte = np.where(mant > 0.5, ex, ex - 1) + 127
    byte = np.clip(np.where(amax > 0, byte, 1), 1, 254)
    scaled = (w * np.exp2(127.0 - byte)[:, None, :]).reshape(k, n).astype(np.float32)
    by_word = np.ascontiguousarray(scaled.reshape(k // 512, 128, 4, n).transpose(0, 1, 3, 2))
    if fmt == "e4m3":
        words = by_word.astype(ml_dtypes.float8_e4m3fn).view(np.uint8)
    else:
        c = by_word.astype(ml_dtypes.float4_e2m1fn).view(np.uint8) & 0xF
        words = c[..., 0::2] | (c[..., 1::2] << 4)
    return np.ascontiguousarray(words), np.ascontiguousarray(byte.astype(np.uint8).reshape(k // 512, 16, n))


def unpack_weight(words, scales, fmt):
    g, p, n, _ = words.shape
    if fmt == "e4m3":
        vals = np.ascontiguousarray(words).view(ml_dtypes.float8_e4m3fn).astype(np.float64)
    else:
        nib = np.empty((g, p, n, 4), np.uint8)
        nib[..., 0::2] = words & 0xF
        nib[..., 1::2] = words >> 4
        vals = E2M1[nib]
    vals = vals * np.repeat(np.exp2(scales.astype(np.float64) - 127.0), 8, axis=1)[..., None]
    return vals.transpose(0, 1, 3, 2).reshape(g * 512, n)


N, D, H = 1024, 512, 1024


def draw0():
    s1, s2 = mx_kscale(D), mx_kscale(D)
    t = mx_kscale(H)
    e1 = np.random.standard_normal((N, D)) * s1
    e2 = np.random.standard_normal((N, D)) * s2
    w1 = np.random.standard_normal((D, H)) / np.sqrt(D) / s1[:, None]
    w2 = np.random.standard_normal((D, H)) / np.sqrt(D) / s2[:, None]
    g1 = (1.0 + 0.1 * np.random.standard_normal(H)) * t
    g2 = (1.0 + 0.1 * np.random.standard_normal(H)) / t
    w1_words, w1_scales = pack_weight(w1, "e4m3")
    w2_words, w2_scales = pack_weight(w2, "e4m3")
    return {"e1": bf(e1), "e2": bf(e2), "w1_words": w1_words, "w1_scales": w1_scales,
            "w2_words": w2_words, "w2_scales": w2_scales, "g1": bf(g1), "g2": bf(g2)}


def gated_projection(e, w_words, w_scales, g):
    return np.tanh(mxq(f64(e), 1, "e4m3") @ unpack_weight(w_words, w_scales, "e4m3")) * f64(g)[None, :]


def core(e1, e2, w1_words, w1_scales, w2_words, w2_scales, g1, g2):
    hidden = w1_words.shape[2]
    m1 = gated_projection(e1, w1_words, w1_scales, g1)
    m2 = gated_projection(e2, w2_words, w2_scales, g2)
    p = (mxq(m1, 1, "e4m3") @ mxq(m2, 1, "e4m3").T) / np.sqrt(hidden)
    q = p - p.T
    return np.maximum(np.tanh(1.5 * q), 0.0)


def e4m3fn_bytes(y):
    return np.clip(np.asarray(y, np.float64), -448.0, 448.0).astype(np.float32).astype(ml_dtypes.float8_e4m3fn).view(np.uint8)


def e4m3fn_values(b):
    return np.asarray(b, np.uint8).view(ml_dtypes.float8_e4m3fn).astype(np.float64)


def setup_inputs():
    d = draw0()
    x0 = np.asarray(d['e2']).astype(np.float64)
    s = (np.max(np.abs(x0), axis=(0,), keepdims=True) / 448.0).astype(np.float32)
    out = {}
    for k, v in d.items():
        if k == 'e2':
            out['e2_bytes'] = e4m3fn_bytes(x0 / s.astype(np.float64))
            out['e2_scale'] = s
        else:
            out[k] = v
    return out


def reference(e1, e2_bytes, e2_scale, w1_words, w1_scales, w2_words, w2_scales, g1, g2):
    return core(e1, e4m3fn_values(e2_bytes) * e2_scale.astype(np.float64), w1_words, w1_scales, w2_words, w2_scales, g1, g2)

@@ -1,0 +1,363 @@
+from contextlib import ExitStack
+
+import concourse.mybir as mybir
+from concourse.masks import make_identity
+
+N, D, H = 1024, 512, 1024
+FLOPS = 2 * (2 * N * D * H) + 2 * N * N * H
+
+F32 = mybir.dt.float32
+BF16 = mybir.dt.bfloat16
+I32 = mybir.dt.int32
+U32 = mybir.dt.uint32
+U8 = mybir.dt.uint8
+FP8 = mybir.dt.float8_e4m3fn
+FP8X4 = mybir.dt.float8_e4m3fn_x4
+ACT = mybir.ActivationFunctionType
+ALU = mybir.AluOpType
+
+P = 128
+PACK = 4
+RUN = 8
+BANK = 512
+CHUNKS = N // P
+PASSES = H // (P * PACK)
+SCORE_SCALE = -1.5 / 32.0
+
+
+def tile_mtgnnantisymmetricgraphlearner_w8_kernel(
+    tc, e1, e2_bytes, e2_scale, w1_words, w1_scales, w2_words, w2_scales, g1, g2, out
+):
+    nc = tc.nc
+    with ExitStack() as ctx:
+        keep = ctx.enter_context(tc.tile_pool(name="keep", bufs=1))
+        work = ctx.enter_context(tc.tile_pool(name="work", bufs=3))
+        results = ctx.enter_context(tc.tile_pool(name="results", bufs=4))
+        tanh_pool = ctx.enter_context(tc.tile_pool(name="tanh", bufs=6))
+        banks = ctx.enter_context(tc.psum_pool(name="banks", bufs=7))
+        gain_bank = ctx.enter_context(tc.psum_pool(name="gain_bank", bufs=1))
+        ctx.enter_context(tc.manual_schedule())
+
+        ident_f32 = keep.tile([P, P], F32, name="ident_f32")
+        pick_rows = keep.tile([P, 2 * PACK], BF16, name="pick_rows")
+        gain_rows = keep.tile([P, PASSES * P], BF16, name="gain_rows")
+        scale_cols = keep.tile([P, PACK], F32, name="scale_cols")
+        scale_spread = keep.tile([P, D], F32, name="scale_spread")
+        gains = gain_bank.tile([P, PASSES * 2 * PACK], F32, name="gains")
+
+        w_raw = [keep.tile([P, H], U32, name="w_raw%d" % a) for a in range(2)]
+        ws_raw = [keep.tile([P, H], U8, name="ws_raw%d" % a) for a in range(2)]
+        w_codes = [[keep.tile([P, BANK], U32, name="w_codes%d%d" % (a, g), align_bytes=64) for g in range(PASSES)] for a in range(2)]
+        w_scale = [keep.tile([P, H], U8, name="w_scale%d" % a, align_bytes=64) for a in range(2)]
+
+        e1_loads = [(0, 1), (1, 1), (2, 2), (4, 4)]
+        e2_loads = [(0, 3), (3, 5)]
+        e1_tiles = [keep.tile([P, n, D], BF16, name="e1_rows%d" % c0) for c0, n in e1_loads]
+        e2_tiles = [keep.tile([P, n, D], U8, name="e2_fp8_rows%d" % c0) for c0, n in e2_loads]
+        e_rows = [{}, {}]
+        e2_fp8 = {}
+        for (c0, n), t in zip(e1_loads, e1_tiles):
+            for j in range(n):
+                e_rows[0][c0 + j] = t[:, j, :]
+        for (c0, n), t in zip(e2_loads, e2_tiles):
+            for j in range(n):
+                e2_fp8[c0 + j] = t[:, j, :]
+
+        m_codes = [[keep.tile([P, N], U32, name="m_codes%d%d" % (a, g), align_bytes=64) for g in range(PASSES)] for a in range(2)]
+        m_scale = [[keep.tile([P, N], U8, name="m_scale%d%d" % (a, g), align_bytes=64) for g in range(PASSES)] for a in range(2)]
+
+        e_turned, e_grouped, e_mx = {}, {}, {}
+        proj, tanh_vals, m_bf16, neg_bf16, neg_mx = {}, {}, {}, {}, {}
+        score, t_vals, t_turned = {}, {}, {}
+
+        def load_rows(tile_ap, src, c0, n):
+            nc.sync.dma_start(out=tile_ap[:], in_=src[c0 * P : (c0 + n) * P, :].rearrange("(c p) k -> p c k", p=P))
+
+        def load_w_scales(a, src):
+            for q in range(4):
+                nc.sync.dma_start(out=ws_raw[a][32 * q : 32 * q + 4, :].bitcast(I32), in_=src[0, 4 * q : 4 * q + 4, :].bitcast(I32))
+
+        def word_view(src):
+            return src[0].rearrange("p n t -> p (n t)").bitcast(I32)
+
+        def order_w_scales(a):
+            nc.vector.tensor_copy(
+                out=w_scale[a][:].bitcast(I32).rearrange("p (g t b r) -> p g t b r", g=PASSES, t=PACK, r=RUN // 4),
+                in_=ws_raw[a][:].bitcast(I32).rearrange("p (g b t r) -> p g t b r", g=PASSES, t=PACK, r=RUN // 4),
+            )
+
+        def order_w_codes(a, g):
+            nc.vector.tensor_copy(
+                out=w_codes[a][g][:].bitcast(I32).rearrange("p (t b r) -> p t b r", t=PACK, r=RUN),
+                in_=w_raw[a][:, g * BANK : (g + 1) * BANK].bitcast(I32).rearrange("p (b t r) -> p t b r", t=PACK, r=RUN),
+            )
+
+        def scale_e2(c):
+            rows = keep.tile([P, D], BF16, name="e2_rows%d" % c)
+            nc.vector.tensor_tensor(out=rows[:], in0=e2_fp8[c].bitcast(FP8), in1=scale_spread[:], op=ALU.mult)
+            e_rows[1][c] = rows[:]
+
+        def turn_e(c, sides):
+            bank = banks.tile([P, BANK], F32, name="bank")
+            for j, a in enumerate(sides):
+                words = e_rows[a][c].bitcast(F32)
+                for u in range(2):
+                    col = (2 * j + u) * P
+                    nc.tensor.transpose(bank[:, col : col + P], words[:, u : D // 2 : 2], ident_f32[:])
+            e_turned[c, sides] = bank
+
+        def group_e(c, sides, on_vector=False):
+            width = len(sides) * 2 * P
+            grouped = work.tile([P, 2 * P * PACK], BF16, name="e_grouped", align_bytes=64)
+            dst = grouped[:].bitcast(F32)[:, 0:width].rearrange("p (j n u) -> p j n u", n=P, u=2)
+            src = e_turned[c, sides][:, 0:width].rearrange("p (j u n) -> p j n u", n=P, u=2)
+            if on_vector:
+                nc.vector.tensor_copy(out=dst, in_=src)
+            else:
+                nc.scalar.copy(out=dst, in_=src)
+            e_grouped[c, sides] = grouped
+
+        def quantize_e(c, sides):
+            width = len(sides) * P
+            codes = keep.tile([P, width], U32, name="e_codes%d%d" % (c, sides[0]), align_bytes=64)
+            scale = keep.tile([P, width], U8, name="e_scale%d%d" % (c, sides[0]), align_bytes=64)
+            nc.vector.quantize_mx(out=codes[:].bitcast(FP8X4), scales=scale[:], in_=e_grouped[c, sides][:, 0 : width * PACK])
+            for j, a in enumerate(sides):
+                e_mx[c, a] = (codes[:, j * P : (j + 1) * P], scale[:, j * P : (j + 1) * P])
+
+        def project(c, a, g):
+            codes, scale = e_mx[c, a]
+            bank = banks.tile([P, BANK], F32, name="bank")
+            for t in range(PACK):
+                nc.tensor.matmul_mx(
+                    out=bank[:, t * P : (t + 1) * P],
+                    lhsT=w_codes[a][g][:, t * P : (t + 1) * P].bitcast(FP8X4),
+                    lhsT_scale=w_scale[a][:, g * BANK + t * P : g * BANK + (t + 1) * P],
+                    rhs=codes.bitcast(FP8X4),
+                    rhs_scale=scale,
+                    start=True,
+                    stop=True,
+                )
+            proj[c, a, g] = bank
+
+        def tanh_proj(c, a, g):
+            vals = tanh_pool.tile([P, P, PACK], F32, name="tanh_vals")
+            nc.scalar.activation(out=vals[:], in_=proj[c, a, g][:].rearrange("p (t n) -> p n t", t=PACK), func=ACT.Tanh)
+            tanh_vals[c, a, g] = vals
+
+        def apply_gain(c, a, g):
+            if g == 0:
+                m_bf16[c, a] = work.tile([P, PASSES * BANK], BF16, name="m_bf16_%d" % a, align_bytes=64)
+            col = (2 * g + a) * PACK
+            nc.vector.tensor_tensor(
+                out=m_bf16[c, a][:, g * BANK : (g + 1) * BANK].rearrange("p (n t) -> p n t", t=PACK),
+                in0=tanh_vals[c, a, g][:],
+                in1=gains[:, col : col + PACK].unsqueeze(1).to_broadcast([P, P, PACK]),
+                op=ALU.mult,
+            )
+
+        def quantize_m(c, a, g):
+            nodes = slice(c * P, (c + 1) * P)
+            nc.vector.quantize_mx(
+                out=m_codes[a][g][:, nodes].bitcast(FP8X4),
+                scales=m_scale[a][g][:, nodes],
+                in_=m_bf16[c, a][:, g * BANK : (g + 1) * BANK],
+            )
+
+        def negate_m1(c):
+            neg = work.tile([P, PASSES * BANK], BF16, name="neg_bf16", align_bytes=64)
+            nc.vector.tensor_scalar(out=neg[:], in0=m_bf16[c, 0][:], scalar1=-1.0, scalar2=None, op0=ALU.mult)
+            neg_bf16[c] = neg
+
+        def quantize_neg(c):
+            codes = work.tile([P, PASSES * P], U32, name="neg_codes", align_bytes=64)
+            scale = work.tile([P, PASSES * P], U8, name="neg_scale", align_bytes=64)
+            nc.vector.quantize_mx(out=codes[:].bitcast(FP8X4), scales=scale[:], in_=neg_bf16[c][:])
+            neg_mx[c] = (codes, scale)
+
+        def spans(c):
+            width = (c + 1) * P
+            return [(c0, min(BANK, width - c0)) for c0 in range(0, width, BANK)]
+
+        def score_pass(c, bank_cols, cols, step, start, stop):
+            g = step % PASSES
+            if step < PASSES:
+                lhs, lhs_scale = (t[:, g * P : (g + 1) * P] for t in neg_mx[c])
+                a = 1
+            else:
+                lhs, lhs_scale = m_codes[1][g][:, c * P : (c + 1) * P], m_scale[1][g][:, c * P : (c + 1) * P]
+                a = 0
+            nc.tensor.matmul_mx(
+                out=bank_cols,
+                lhsT=lhs.bitcast(FP8X4),
+                lhsT_scale=lhs_scale,
+                rhs=m_codes[a][g][:, cols].bitcast(FP8X4),
+                rhs_scale=m_scale[a][g][:, cols],
+                start=start,
+                stop=stop,
+            )
+
+        def score_span(c, c0, width):
+            bank = banks.tile([P, BANK], F32, name="bank")
+            groups = [(0, 2 * P), (2 * P, P)] if width == 3 * P else [(0, width)]
+            for off, n in groups:
+                for step in range(2 * PASSES):
+                    score_pass(c, bank[:, off : off + n], slice(c0 + off, c0 + off + n), step, step == 0, step == 2 * PASSES - 1)
+            score[c, c0] = bank
+
+        def tanh_span(c, c0, width):
+            if c0 == 0:
+                t_vals[c] = work.tile([P, N], F32, name="t_vals")
+            nc.scalar.activation(out=t_vals[c][:, c0 : c0 + width], in_=score[c, c0][:, 0:width], func=ACT.Tanh, scale=SCORE_SCALE)
+
+        def store_lower(c, c0, width, on_vector):
+            res = results.tile([P, N], F32, name="lower")
+            if on_vector:
+                nc.vector.tensor_scalar(out=res[:, 0:width], in0=t_vals[c][:, c0 : c0 + width], scalar1=0.0, scalar2=None, op0=ALU.max)
+            else:
+                nc.scalar.activation(out=res[:, 0:width], in_=t_vals[c][:, c0 : c0 + width], func=ACT.Relu)
+            nc.sync.dma_start(out=out[c * P : (c + 1) * P, c0 : c0 + width], in_=res[:, 0:width])
+
+        def mirror_spans(c):
+            return [(i0, min(4, c - i0)) for i0 in range(0, c, 4)]
+
+        def turn_t(c, i0, n):
+            bank = banks.tile([P, BANK], F32, name="bank")
+            for i in range(n):
+                nc.tensor.transpose(bank[:, i * P : (i + 1) * P], t_vals[c][:, (i0 + i) * P : (i0 + i + 1) * P], ident_f32[:])
+            t_turned[c, i0] = bank
+
+        def store_upper(c, i0, n, on_vector):
+            res = results.tile([P, BANK], F32, name="upper")
+            src = t_turned[c, i0][:, 0 : n * P]
+            if on_vector:
+                nc.vector.tensor_scalar(out=res[:, 0 : n * P], in0=src, scalar1=-1.0, scalar2=0.0, op0=ALU.mult, op1=ALU.max)
+            else:
+                nc.scalar.activation(out=res[:, 0 : n * P], in_=src, func=ACT.Relu, scale=-1.0)
+            nc.sync.dma_start(
+                out=out[i0 * P : (i0 + n) * P, c * P : (c + 1) * P].rearrange("(i p) n -> p i n", p=P),
+                in_=res[:, 0 : n * P].rearrange("p (i n) -> p i n", n=P),
+            )
+
+        make_identity(nc, ident_f32[:])
+        nc.vector.memset(ws_raw[0][:].bitcast(I32), 0)
+        nc.vector.memset(gain_rows[:], 0.0)
+        nc.vector.memset(ws_raw[1][:].bitcast(I32), 0)
+        for a, gain in enumerate((g1, g2)):
+            nc.gpsimd.dma_start(
+                out=gain_rows[a * PACK : (a + 1) * PACK, :].rearrange("t (q r) -> t q r", r=RUN),
+                in_=gain.rearrange("(q t r) -> t q r", t=PACK, r=RUN),
+            )
+        nc.vector.tensor_copy(out=pick_rows[:], in_=ident_f32[:, 0 : 2 * PACK])
+
+        load_rows(e1_tiles[0], e1, *e1_loads[0])
+        nc.sync.dma_start(out=scale_cols[:], in_=e2_scale.rearrange("o (n m) -> n (o m)", m=PACK))
+        nc.sync.dma_start(out=w_raw[0][:].bitcast(I32), in_=word_view(w1_words))
+        load_w_scales(0, w1_scales)
+        load_rows(e2_tiles[0], e2_bytes, *e2_loads[0])
+        load_rows(e1_tiles[1], e1, *e1_loads[1])
+        nc.sync.dma_start(out=w_raw[1][:].bitcast(I32), in_=word_view(w2_words))
+        load_w_scales(1, w2_scales)
+        load_rows(e1_tiles[2], e1, *e1_loads[2])
+        load_rows(e2_tiles[1], e2_bytes, *e2_loads[1])
+        load_rows(e1_tiles[3], e1, *e1_loads[3])
+
+        turn_e(0, (0,))
+        group_e(0, (0,), on_vector=True)
+        spread_bank = banks.tile([P, BANK], F32, name="bank")
+        for t in range(PACK):
+            nc.tensor.transpose(spread_bank[:, t * P : (t + 1) * P], scale_cols[:, t : t + 1].to_broadcast([P, P]), ident_f32[:])
+        nc.scalar.activation(
+            out=scale_spread[:].rearrange("p (n t) -> p n t", t=PACK),
+            in_=spread_bank[:].rearrange("p (t n) -> p n t", t=PACK),
+            func=ACT.Copy,
+        )
+        order_w_codes(0, 0)
+        quantize_e(0, (0,))
+        order_w_scales(0)
+        order_w_codes(0, 1)
+        scale_e2(0)
+        scale_e2(1)
+        scale_e2(2)
+
+        both = (0, 1)
+        last = CHUNKS - 1
+        for c in range(CHUNKS):
+            for g in range(PASSES):
+                project(c, 0, g)
+            if c == 0:
+                for g in range(PASSES):
+                    nc.tensor.matmul(
+                        gains[:, g * 2 * PACK : (g + 1) * 2 * PACK],
+                        lhsT=gain_rows[:, g * P : (g + 1) * P],
+                        rhs=pick_rows[:],
+                        start=True,
+                        stop=True,
+                    )
+                turn_e(0, (1,))
+            tanh_proj(c, 0, 0)
+            if c == 0:
+                group_e(0, (1,))
+            tanh_proj(c, 0, 1)
+            if c < last:
+                turn_e(c + 1, both)
+            for i0, n in mirror_spans(c - 2):
+                turn_t(c - 2, i0, n)
+            if c < last:
+                group_e(c + 1, both)
+            for i0, n in mirror_spans(c - 2):
+                store_upper(c - 2, i0, n, on_vector=False)
+            if 2 <= c <= 5:
+                store_lower(c - 2, 0, (c - 1) * P, on_vector=False)
+
+            apply_gain(c, 0, 0)
+            if c == 0:
+                quantize_e(0, (1,))
+                order_w_scales(1)
+                order_w_codes(1, 0)
+                order_w_codes(1, 1)
+            apply_gain(c, 0, 1)
+            if 1 <= c <= last - 2:
+                scale_e2(c + 2)
+            if c >= 6:
+                store_lower(c - 2, 0, (c - 1) * P, on_vector=True)
+            negate_m1(c)
+            quantize_m(c, 0, 0)
+            quantize_m(c, 0, 1)
+            if c < last:
+                quantize_e(c + 1, both)
+            else:
+                quantize_neg(c)
+
+            for g in range(PASSES):
+                project(c, 1, g)
+            for g in range(PASSES):
+                tanh_proj(c, 1, g)
+            if c >= 1:
+                for c0, width in spans(c - 1):
+                    score_span(c - 1, c0, width)
+                for c0, width in spans(c - 1):
+                    tanh_span(c - 1, c0, width)
+
+            apply_gain(c, 1, 0)
+            apply_gain(c, 1, 1)
+            if c < last:
+                quantize_neg(c)
+            quantize_m(c, 1, 0)
+            quantize_m(c, 1, 1)
+
+        for i0, n in mirror_spans(last - 1):
+            turn_t(last - 1, i0, n)
+        for i0, n in mirror_spans(last - 1):
+            store_upper(last - 1, i0, n, on_vector=False)
+        store_lower(last - 1, 0, last * P, on_vector=True)
+        for c0, width in spans(last):
+            score_span(last, c0, width)
+        for c0, width in spans(last):
+            tanh_span(last, c0, width)
+        for i0, n in mirror_spans(last):
+            turn_t(last, i0, n)
+        store_lower(last, 0, BANK, on_vector=True)
+        store_upper(last, 0, 4, on_vector=True)
+        store_lower(last, BANK, BANK, on_vector=True)
+        store_upper(last, 4, 3, on_vector=False)

@@ -21,6 +21,8 @@ PACK = 4
 RUN = 8
 BANK = 512
 CHUNKS = N // P
+PAIR = 2 * P
+PAIRS = CHUNKS // 2
 PASSES = H // (P * PACK)
 SCORE_SCALE = -1.5 / 32.0
 
@@ -33,7 +35,7 @@ def tile_mtgnnantisymmetricgraphlearner_w8_kernel(
         keep = ctx.enter_context(tc.tile_pool(name="keep", bufs=1))
         work = ctx.enter_context(tc.tile_pool(name="work", bufs=3))
         results = ctx.enter_context(tc.tile_pool(name="results", bufs=4))
-        tanh_pool = ctx.enter_context(tc.tile_pool(name="tanh", bufs=6))
+        tanh_pool = ctx.enter_context(tc.tile_pool(name="tanh", bufs=10))
         banks = ctx.enter_context(tc.psum_pool(name="banks", bufs=7))
         gain_bank = ctx.enter_context(tc.psum_pool(name="gain_bank", bufs=1))
         ctx.enter_context(tc.manual_schedule())
@@ -42,7 +44,7 @@ def tile_mtgnnantisymmetricgraphlearner_w8_kernel(
         pick_rows = keep.tile([P, 2 * PACK], BF16, name="pick_rows")
         gain_rows = keep.tile([P, PASSES * P], BF16, name="gain_rows")
         scale_cols = keep.tile([P, PACK], F32, name="scale_cols")
-        scale_spread = keep.tile([P, D], F32, name="scale_spread")
+        scale_spread = keep.tile([P, 2 * D], F32, name="scale_spread")
         gains = gain_bank.tile([P, PASSES * 2 * PACK], F32, name="gains")
 
         w_raw = [keep.tile([P, H], U32, name="w_raw%d" % a) for a in range(2)]
@@ -50,28 +52,28 @@ def tile_mtgnnantisymmetricgraphlearner_w8_kernel(
         w_codes = [[keep.tile([P, BANK], U32, name="w_codes%d%d" % (a, g), align_bytes=64) for g in range(PASSES)] for a in range(2)]
         w_scale = [keep.tile([P, H], U8, name="w_scale%d" % a, align_bytes=64) for a in range(2)]
 
-        e1_loads = [(0, 1), (1, 1), (2, 2), (4, 4)]
-        e2_loads = [(0, 3), (3, 5)]
-        e1_tiles = [keep.tile([P, n, D], BF16, name="e1_rows%d" % c0) for c0, n in e1_loads]
-        e2_tiles = [keep.tile([P, n, D], U8, name="e2_fp8_rows%d" % c0) for c0, n in e2_loads]
+        e1_loads = [(0, 2), (2, 2), (4, 4)]
+        e2_loads = [(0, 2), (2, 2), (4, 4)]
+        e1_tiles = [keep.tile([P, n * D], BF16, name="e1_rows%d" % c0) for c0, n in e1_loads]
+        e2_tiles = [keep.tile([P, n * D], U8, name="e2_fp8_rows%d" % c0) for c0, n in e2_loads]
         e_rows = [{}, {}]
         e2_fp8 = {}
         for (c0, n), t in zip(e1_loads, e1_tiles):
-            for j in range(n):
-                e_rows[0][c0 + j] = t[:, j, :]
+            for j in range(0, n, 2):
+                e_rows[0][(c0 + j) // 2] = t[:, j * D : (j + 2) * D]
         for (c0, n), t in zip(e2_loads, e2_tiles):
-            for j in range(n):
-                e2_fp8[c0 + j] = t[:, j, :]
+            for j in range(0, n, 2):
+                e2_fp8[(c0 + j) // 2] = t[:, j * D : (j + 2) * D]
 
         m_codes = [[keep.tile([P, N], U32, name="m_codes%d%d" % (a, g), align_bytes=64) for g in range(PASSES)] for a in range(2)]
         m_scale = [[keep.tile([P, N], U8, name="m_scale%d%d" % (a, g), align_bytes=64) for g in range(PASSES)] for a in range(2)]
 
         e_turned, e_grouped, e_mx = {}, {}, {}
         proj, tanh_vals, m_bf16, neg_bf16, neg_mx = {}, {}, {}, {}, {}
-        score, t_vals, t_turned = {}, {}, {}
+        score, t_vals, t_turned, row_res = {}, {}, {}, {}
 
         def load_rows(tile_ap, src, c0, n):
-            nc.sync.dma_start(out=tile_ap[:], in_=src[c0 * P : (c0 + n) * P, :].rearrange("(c p) k -> p c k", p=P))
+            nc.sync.dma_start(out=tile_ap[:].rearrange("p (c k) -> p c k", k=D), in_=src[c0 * P : (c0 + n) * P, :].rearrange("(c p) k -> p c k", p=P))
 
         def load_w_scales(a, src):
             for q in range(4):
@@ -92,45 +94,44 @@ def tile_mtgnnantisymmetricgraphlearner_w8_kernel(
                 in_=w_raw[a][:, g * BANK : (g + 1) * BANK].bitcast(I32).rearrange("p (b t r) -> p t b r", t=PACK, r=RUN),
             )
 
-        def scale_e2(c):
-            rows = keep.tile([P, D], BF16, name="e2_rows%d" % c)
-            nc.vector.tensor_tensor(out=rows[:], in0=e2_fp8[c].bitcast(FP8), in1=scale_spread[:], op=ALU.mult)
-            e_rows[1][c] = rows[:]
+        def scale_e2(pair):
+            rows = work.tile([P, 2 * D], BF16, name="e2_rows")
+            nc.vector.tensor_tensor(out=rows[:], in0=e2_fp8[pair].bitcast(FP8), in1=scale_spread[:], op=ALU.mult)
+            e_rows[1][pair] = rows[:]
 
-        def turn_e(c, sides):
+        def turn_e(pair, a):
             bank = banks.tile([P, BANK], F32, name="bank")
-            for j, a in enumerate(sides):
-                words = e_rows[a][c].bitcast(F32)
+            words = e_rows[a][pair].bitcast(F32)
+            for j in range(2):
                 for u in range(2):
                     col = (2 * j + u) * P
-                    nc.tensor.transpose(bank[:, col : col + P], words[:, u : D // 2 : 2], ident_f32[:])
-            e_turned[c, sides] = bank
+                    nc.tensor.transpose(bank[:, col : col + P], words[:, j * 2 * P + u : (j + 1) * 2 * P : 2], ident_f32[:])
+            e_turned[pair, a] = bank
 
-        def group_e(c, sides, on_vector=False):
-            width = len(sides) * 2 * P
-            grouped = work.tile([P, 2 * P * PACK], BF16, name="e_grouped", align_bytes=64)
-            dst = grouped[:].bitcast(F32)[:, 0:width].rearrange("p (j n u) -> p j n u", n=P, u=2)
-            src = e_turned[c, sides][:, 0:width].rearrange("p (j u n) -> p j n u", n=P, u=2)
+        def group_e(pair, a, on_vector=False):
+            if a == 0:
+                e_grouped[pair] = work.tile([P, 2 * PAIR * PACK], BF16, name="e_grouped", align_bytes=64)
+            dst = e_grouped[pair][:].bitcast(F32)[:, a * BANK : (a + 1) * BANK].rearrange("p (j n u) -> p j n u", n=P, u=2)
+            src = e_turned[pair, a][:].rearrange("p (j u n) -> p j n u", n=P, u=2)
             if on_vector:
                 nc.vector.tensor_copy(out=dst, in_=src)
             else:
                 nc.scalar.copy(out=dst, in_=src)
-            e_grouped[c, sides] = grouped
 
-        def quantize_e(c, sides):
-            width = len(sides) * P
-            codes = keep.tile([P, width], U32, name="e_codes%d%d" % (c, sides[0]), align_bytes=64)
-            scale = keep.tile([P, width], U8, name="e_scale%d%d" % (c, sides[0]), align_bytes=64)
-            nc.vector.quantize_mx(out=codes[:].bitcast(FP8X4), scales=scale[:], in_=e_grouped[c, sides][:, 0 : width * PACK])
-            for j, a in enumerate(sides):
-                e_mx[c, a] = (codes[:, j * P : (j + 1) * P], scale[:, j * P : (j + 1) * P])
+        def quantize_e(pair, a0, n):
+            codes = keep.tile([P, n * PAIR], U32, name="e_codes%d%d" % (pair, a0), align_bytes=64)
+            scale = keep.tile([P, n * PAIR], U8, name="e_scale%d%d" % (pair, a0), align_bytes=64)
+            nc.vector.quantize_mx(out=codes[:].bitcast(FP8X4), scales=scale[:], in_=e_grouped[pair][:, a0 * PAIR * PACK : (a0 + n) * PAIR * PACK])
+            for j in range(n):
+                e_mx[pair, a0 + j] = (codes[:, j * PAIR : (j + 1) * PAIR], scale[:, j * PAIR : (j + 1) * PAIR])
 
-        def project(c, a, g):
-            codes, scale = e_mx[c, a]
+        def project(pair, a, g, u):
+            codes, scale = e_mx[pair, a]
             bank = banks.tile([P, BANK], F32, name="bank")
-            for t in range(PACK):
+            for e in range(2):
+                t = 2 * u + e
                 nc.tensor.matmul_mx(
-                    out=bank[:, t * P : (t + 1) * P],
+                    out=bank[:, e * PAIR : (e + 1) * PAIR],
                     lhsT=w_codes[a][g][:, t * P : (t + 1) * P].bitcast(FP8X4),
                     lhsT_scale=w_scale[a][:, g * BANK + t * P : g * BANK + (t + 1) * P],
                     rhs=codes.bitcast(FP8X4),
@@ -138,42 +139,60 @@ def tile_mtgnnantisymmetricgraphlearner_w8_kernel(
                     start=True,
                     stop=True,
                 )
-            proj[c, a, g] = bank
+            proj[pair, a, g, u] = bank
 
-        def tanh_proj(c, a, g):
-            vals = tanh_pool.tile([P, P, PACK], F32, name="tanh_vals")
-            nc.scalar.activation(out=vals[:], in_=proj[c, a, g][:].rearrange("p (t n) -> p n t", t=PACK), func=ACT.Tanh)
-            tanh_vals[c, a, g] = vals
+        def tanh_proj(pair, a, g, u):
+            if u == 0:
+                tanh_vals[pair, a, g] = tanh_pool.tile([P, 2, PAIR, 2], F32, name="tanh_vals")
+            nc.scalar.activation(
+                out=tanh_vals[pair, a, g][:, u, :, :], in_=proj[pair, a, g, u][:].rearrange("p (e n) -> p n e", e=2), func=ACT.Tanh
+            )
 
-        def apply_gain(c, a, g):
+        def project_side(pair, a):
+            for g in range(PASSES):
+                for u in range(2):
+                    project(pair, a, g, u)
+            for g in range(PASSES):
+                for u in range(2):
+                    tanh_proj(pair, a, g, u)
+
+        def apply_gain(c, n, a, g):
+            pair, lo = c // 2, (c % 2) * P
             if g == 0:
-                m_bf16[c, a] = work.tile([P, PASSES * BANK], BF16, name="m_bf16_%d" % a, align_bytes=64)
+                m_bf16[c, a] = work.tile([P, PASSES * PAIR * PACK], BF16, name="m_bf16_%d" % a, align_bytes=64)
             col = (2 * g + a) * PACK
+            width = n * P * PACK
             nc.vector.tensor_tensor(
-                out=m_bf16[c, a][:, g * BANK : (g + 1) * BANK].rearrange("p (n t) -> p n t", t=PACK),
-                in0=tanh_vals[c, a, g][:],
-                in1=gains[:, col : col + PACK].unsqueeze(1).to_broadcast([P, P, PACK]),
+                out=m_bf16[c, a][:, g * width : (g + 1) * width].rearrange("p (n u e) -> p n u e", u=2, e=2),
+                in0=tanh_vals[pair, a, g][:, :, lo : lo + n * P, :].rearrange("p u n e -> p n u e"),
+                in1=gains[:, col : col + PACK].rearrange("p (u e) -> p u e", e=2).unsqueeze(1).to_broadcast([P, n * P, 2, 2]),
                 op=ALU.mult,
             )
 
-        def quantize_m(c, a, g):
-            nodes = slice(c * P, (c + 1) * P)
+        def quantize_m(c, n, a, g):
+            nodes = slice(c * P, (c + n) * P)
+            width = n * P * PACK
             nc.vector.quantize_mx(
                 out=m_codes[a][g][:, nodes].bitcast(FP8X4),
                 scales=m_scale[a][g][:, nodes],
-                in_=m_bf16[c, a][:, g * BANK : (g + 1) * BANK],
+                in_=m_bf16[c, a][:, g * width : (g + 1) * width],
             )
 
-        def negate_m1(c):
-            neg = work.tile([P, PASSES * BANK], BF16, name="neg_bf16", align_bytes=64)
-            nc.vector.tensor_scalar(out=neg[:], in0=m_bf16[c, 0][:], scalar1=-1.0, scalar2=None, op0=ALU.mult)
+        def negate_m1(c, n):
+            width = PASSES * n * P * PACK
+            neg = work.tile([P, PASSES * PAIR * PACK], BF16, name="neg_bf16", align_bytes=64)
+            nc.vector.tensor_scalar(out=neg[:, 0:width], in0=m_bf16[c, 0][:, 0:width], scalar1=-1.0, scalar2=None, op0=ALU.mult)
             neg_bf16[c] = neg
 
-        def quantize_neg(c):
-            codes = work.tile([P, PASSES * P], U32, name="neg_codes", align_bytes=64)
-            scale = work.tile([P, PASSES * P], U8, name="neg_scale", align_bytes=64)
-            nc.vector.quantize_mx(out=codes[:].bitcast(FP8X4), scales=scale[:], in_=neg_bf16[c][:])
-            neg_mx[c] = (codes, scale)
+        def quantize_neg(c, n):
+            width = PASSES * n * P
+            codes = work.tile([P, PASSES * PAIR], U32, name="neg_codes", align_bytes=64)
+            scale = work.tile([P, PASSES * PAIR], U8, name="neg_scale", align_bytes=64)
+            nc.vector.quantize_mx(out=codes[:, 0:width].bitcast(FP8X4), scales=scale[:, 0:width], in_=neg_bf16[c][:, 0 : width * PACK])
+            for j in range(n):
+                for g in range(PASSES):
+                    cols = slice((g * n + j) * P, (g * n + j + 1) * P)
+                    neg_mx[c + j, g] = (codes[:, cols], scale[:, cols])
 
         def spans(c):
             width = (c + 1) * P
@@ -182,7 +201,7 @@ def tile_mtgnnantisymmetricgraphlearner_w8_kernel(
         def score_pass(c, bank_cols, cols, step, start, stop):
             g = step % PASSES
             if step < PASSES:
-                lhs, lhs_scale = (t[:, g * P : (g + 1) * P] for t in neg_mx[c])
+                lhs, lhs_scale = neg_mx[c, g]
                 a = 1
             else:
                 lhs, lhs_scale = m_codes[1][g][:, c * P : (c + 1) * P], m_scale[1][g][:, c * P : (c + 1) * P]
@@ -207,7 +226,7 @@ def tile_mtgnnantisymmetricgraphlearner_w8_kernel(
 
         def tanh_span(c, c0, width):
             if c0 == 0:
-                t_vals[c] = work.tile([P, N], F32, name="t_vals")
+                t_vals[c] = results.tile([P, N], F32, name="t_vals")
             nc.scalar.activation(out=t_vals[c][:, c0 : c0 + width], in_=score[c, c0][:, 0:width], func=ACT.Tanh, scale=SCORE_SCALE)
 
         def store_lower(c, c0, width, on_vector):
@@ -217,6 +236,73 @@ def tile_mtgnnantisymmetricgraphlearner_w8_kernel(
             else:
                 nc.scalar.activation(out=res[:, 0:width], in_=t_vals[c][:, c0 : c0 + width], func=ACT.Relu)
             nc.sync.dma_start(out=out[c * P : (c + 1) * P, c0 : c0 + width], in_=res[:, 0:width])
+
+        def score_row(c):
+            for c0, width in spans(c):
+                score_span(c, c0, width)
+            for c0, width in spans(c):
+                tanh_span(c, c0, width)
+
+        def relu_neg(dst, src, on_vector):
+            if on_vector:
+                nc.vector.tensor_scalar(out=dst, in0=src, scalar1=-1.0, scalar2=0.0, op0=ALU.mult, op1=ALU.max)
+            else:
+                nc.scalar.activation(out=dst, in_=src, func=ACT.Relu, scale=-1.0)
+
+        def mirror_pair(pair):
+            c = 2 * pair
+            turned = []
+            for i0 in range(0, c, 2):
+                bank = banks.tile([P, BANK], F32, name="bank")
+                for i in range(2):
+                    for j in range(2):
+                        col = (2 * i + j) * P
+                        nc.tensor.transpose(bank[:, col : col + P], t_vals[c + j][:, (i0 + i) * P : (i0 + i + 1) * P], ident_f32[:])
+                turned.append((i0, bank))
+            inner = banks.tile([P, BANK], F32, name="bank")
+            nc.tensor.transpose(inner[:, 0:P], t_vals[c + 1][:, c * P : (c + 1) * P], ident_f32[:])
+            for i0, bank in turned:
+                res = results.tile([P, BANK], F32, name="upper")
+                relu_neg(res[:], bank[:], False)
+                nc.sync.dma_start(
+                    out=out[i0 * P : (i0 + 2) * P, c * P : (c + 2) * P].rearrange("(i p) n -> p i n", p=P),
+                    in_=res[:].rearrange("p (i n) -> p i n", n=PAIR),
+                )
+            res = results.tile([P, BANK], F32, name="upper")
+            relu_neg(res[:, 0:P], inner[:, 0:P], False)
+            nc.sync.dma_start(out=out[c * P : (c + 1) * P, (c + 1) * P : (c + 2) * P], in_=res[:, 0:P])
+
+        def side_one(c, n):
+            apply_gain(c, n, 0, 0)
+            apply_gain(c, n, 0, 1)
+            quantize_m(c, n, 0, 0)
+            negate_m1(c, n)
+            quantize_m(c, n, 0, 1)
+
+        def side_two(c, n):
+            apply_gain(c, n, 1, 0)
+            quantize_neg(c, n)
+            apply_gain(c, n, 1, 1)
+            quantize_m(c, n, 1, 0)
+            quantize_m(c, n, 1, 1)
+
+        def finish_nodes(c, n):
+            apply_gain(c, n, 0, 0)
+            apply_gain(c, n, 0, 1)
+            apply_gain(c, n, 1, 0)
+            negate_m1(c, n)
+            quantize_m(c, n, 0, 0)
+            quantize_m(c, n, 0, 1)
+            apply_gain(c, n, 1, 1)
+            quantize_neg(c, n)
+            quantize_m(c, n, 1, 0)
+            quantize_m(c, n, 1, 1)
+
+        def mirror_row(c):
+            for i0, n in mirror_spans(c):
+                turn_t(c, i0, n)
+            for i0, n in mirror_spans(c):
+                store_upper(c, i0, n, on_vector=False)
 
         def mirror_spans(c):
             return [(i0, min(4, c - i0)) for i0 in range(0, c, 4)]
@@ -250,114 +336,136 @@ def tile_mtgnnantisymmetricgraphlearner_w8_kernel(
             )
         nc.vector.tensor_copy(out=pick_rows[:], in_=ident_f32[:, 0 : 2 * PACK])
 
-        load_rows(e1_tiles[0], e1, *e1_loads[0])
         nc.sync.dma_start(out=scale_cols[:], in_=e2_scale.rearrange("o (n m) -> n (o m)", m=PACK))
+        load_rows(e1_tiles[0], e1, *e1_loads[0])
         nc.sync.dma_start(out=w_raw[0][:].bitcast(I32), in_=word_view(w1_words))
         load_w_scales(0, w1_scales)
         load_rows(e2_tiles[0], e2_bytes, *e2_loads[0])
         load_rows(e1_tiles[1], e1, *e1_loads[1])
+        load_rows(e2_tiles[1], e2_bytes, *e2_loads[1])
         nc.sync.dma_start(out=w_raw[1][:].bitcast(I32), in_=word_view(w2_words))
         load_w_scales(1, w2_scales)
+        load_rows(e2_tiles[2], e2_bytes, *e2_loads[2])
         load_rows(e1_tiles[2], e1, *e1_loads[2])
-        load_rows(e2_tiles[1], e2_bytes, *e2_loads[1])
-        load_rows(e1_tiles[3], e1, *e1_loads[3])
 
-        turn_e(0, (0,))
-        group_e(0, (0,), on_vector=True)
         spread_bank = banks.tile([P, BANK], F32, name="bank")
         for t in range(PACK):
             nc.tensor.transpose(spread_bank[:, t * P : (t + 1) * P], scale_cols[:, t : t + 1].to_broadcast([P, P]), ident_f32[:])
         nc.scalar.activation(
-            out=scale_spread[:].rearrange("p (n t) -> p n t", t=PACK),
-            in_=spread_bank[:].rearrange("p (t n) -> p n t", t=PACK),
+            out=scale_spread[:].rearrange("p (j n t) -> p j n t", j=2, t=PACK),
+            in_=spread_bank[:].rearrange("p (t n) -> p n t", t=PACK).unsqueeze(1).to_broadcast([P, 2, P, PACK]),
             func=ACT.Copy,
         )
+        turn_e(0, 0)
+        group_e(0, 0)
         order_w_codes(0, 0)
-        quantize_e(0, (0,))
-        order_w_scales(0)
         order_w_codes(0, 1)
+        order_w_scales(0)
+        quantize_e(0, 0, 1)
         scale_e2(0)
         scale_e2(1)
+        for g in range(PASSES):
+            for u in range(2):
+                project(0, 0, g, u)
+        for g in range(PASSES):
+            nc.tensor.matmul(
+                gains[:, g * 2 * PACK : (g + 1) * 2 * PACK],
+                lhsT=gain_rows[:, g * P : (g + 1) * P],
+                rhs=pick_rows[:],
+                start=True,
+                stop=True,
+            )
+        turn_e(0, 1)
+        turn_e(1, 0)
+        turn_e(1, 1)
+        for g in range(PASSES):
+            for u in range(2):
+                tanh_proj(0, 0, g, u)
+        group_e(0, 1)
+        group_e(1, 0)
+        group_e(1, 1)
+        order_w_codes(1, 0)
+        order_w_codes(1, 1)
+        order_w_scales(1)
+        apply_gain(0, 2, 0, 0)
+        quantize_e(0, 1, 1)
+        apply_gain(0, 2, 0, 1)
+        quantize_e(1, 0, 2)
         scale_e2(2)
-
-        both = (0, 1)
+        negate_m1(0, 2)
+        quantize_m(0, 2, 0, 0)
+        quantize_m(0, 2, 0, 1)
+        project_side(0, 1)
+        project_side(1, 0)
+        turn_e(2, 0)
+        turn_e(2, 1)
+        group_e(2, 0)
+        group_e(2, 1)
+        scale_e2(3)
+        apply_gain(0, 2, 1, 0)
+        quantize_neg(0, 2)
+        apply_gain(0, 2, 1, 1)
+        quantize_e(2, 0, 2)
+        quantize_m(0, 2, 1, 0)
+        quantize_m(0, 2, 1, 1)
+        project_side(1, 1)
+        turn_e(3, 0)
+        turn_e(3, 1)
+        group_e(3, 0)
+        group_e(3, 1)
+        project_side(2, 0)
+        score_row(0)
+        score_row(1)
+        apply_gain(2, 2, 0, 0)
+        apply_gain(2, 2, 0, 1)
+        quantize_e(3, 0, 2)
+        negate_m1(2, 2)
+        quantize_m(2, 2, 0, 0)
+        quantize_m(2, 2, 0, 1)
+        project_side(2, 1)
+        mirror_pair(0)
+        store_lower(0, 0, P, on_vector=False)
+        store_lower(1, 0, 2 * P, on_vector=False)
+        project_side(3, 0)
+        side_two(2, 2)
+        score_row(2)
+        score_row(3)
+        project_side(3, 1)
         last = CHUNKS - 1
-        for c in range(CHUNKS):
-            for g in range(PASSES):
-                project(c, 0, g)
-            if c == 0:
-                for g in range(PASSES):
-                    nc.tensor.matmul(
-                        gains[:, g * 2 * PACK : (g + 1) * 2 * PACK],
-                        lhsT=gain_rows[:, g * P : (g + 1) * P],
-                        rhs=pick_rows[:],
-                        start=True,
-                        stop=True,
-                    )
-                turn_e(0, (1,))
-            tanh_proj(c, 0, 0)
-            if c == 0:
-                group_e(0, (1,))
-            tanh_proj(c, 0, 1)
-            if c < last:
-                turn_e(c + 1, both)
-            for i0, n in mirror_spans(c - 2):
-                turn_t(c - 2, i0, n)
-            if c < last:
-                group_e(c + 1, both)
-            for i0, n in mirror_spans(c - 2):
-                store_upper(c - 2, i0, n, on_vector=False)
-            if 2 <= c <= 5:
-                store_lower(c - 2, 0, (c - 1) * P, on_vector=False)
-
-            apply_gain(c, 0, 0)
-            if c == 0:
-                quantize_e(0, (1,))
-                order_w_scales(1)
-                order_w_codes(1, 0)
-                order_w_codes(1, 1)
-            apply_gain(c, 0, 1)
-            if 1 <= c <= last - 2:
-                scale_e2(c + 2)
-            if c >= 6:
-                store_lower(c - 2, 0, (c - 1) * P, on_vector=True)
-            negate_m1(c)
-            quantize_m(c, 0, 0)
-            quantize_m(c, 0, 1)
-            if c < last:
-                quantize_e(c + 1, both)
-            else:
-                quantize_neg(c)
-
-            for g in range(PASSES):
-                project(c, 1, g)
-            for g in range(PASSES):
-                tanh_proj(c, 1, g)
-            if c >= 1:
-                for c0, width in spans(c - 1):
-                    score_span(c - 1, c0, width)
-                for c0, width in spans(c - 1):
-                    tanh_span(c - 1, c0, width)
-
-            apply_gain(c, 1, 0)
-            apply_gain(c, 1, 1)
-            if c < last:
-                quantize_neg(c)
-            quantize_m(c, 1, 0)
-            quantize_m(c, 1, 1)
-
-        for i0, n in mirror_spans(last - 1):
-            turn_t(last - 1, i0, n)
-        for i0, n in mirror_spans(last - 1):
-            store_upper(last - 1, i0, n, on_vector=False)
-        store_lower(last - 1, 0, last * P, on_vector=True)
+        finish_nodes(4, 1)
+        mirror_pair(1)
+        store_lower(2, 0, 3 * P, on_vector=False)
+        store_lower(3, 0, 4 * P, on_vector=False)
+        score_row(4)
+        store_lower(4, 0, 5 * P, on_vector=False)
+        finish_nodes(5, 1)
+        score_row(5)
+        mirror_row(4)
+        store_lower(5, 0, 6 * P, on_vector=False)
+        mirror_row(5)
+        finish_nodes(6, 1)
+        score_row(6)
+        store_lower(6, 0, 7 * P, on_vector=False)
+        mirror_row(6)
+        apply_gain(last, 1, 0, 0)
+        apply_gain(last, 1, 0, 1)
+        apply_gain(last, 1, 1, 0)
+        negate_m1(last, 1)
+        quantize_m(last, 1, 0, 0)
+        quantize_m(last, 1, 0, 1)
+        quantize_neg(last, 1)
+        quantize_m(last, 1, 1, 0)
+        apply_gain(last, 1, 1, 1)
+        quantize_m(last, 1, 1, 1)
         for c0, width in spans(last):
-            score_span(last, c0, width)
+            score[last, c0] = banks.tile([P, BANK], F32, name="bank")
+        for c0, step in [(0, 0), (0, 1), (0, 2), (BANK, 0), (BANK, 2), (0, 3), (BANK, 1), (BANK, 3)]:
+            score_pass(last, score[last, c0][:], slice(c0, c0 + BANK), step, step == 0, step == 3)
         for c0, width in spans(last):
             tanh_span(last, c0, width)
         for i0, n in mirror_spans(last):
             turn_t(last, i0, n)
         store_lower(last, 0, BANK, on_vector=True)
-        store_upper(last, 0, 4, on_vector=True)
         store_lower(last, BANK, BANK, on_vector=True)
-        store_upper(last, 4, 3, on_vector=False)
+        store_upper(last, 0, 4, on_vector=False)
+        store_upper(last, 4, 3, on_vector=True)

@@ -45,6 +45,8 @@ def tile_mtgnnantisymmetricgraphlearner_w8_kernel(
         gain_rows = keep.tile([P, PASSES * P], BF16, name="gain_rows")
         scale_cols = keep.tile([P, PACK], F32, name="scale_cols")
         scale_spread = keep.tile([P, 2 * D], F32, name="scale_spread")
+        gain_spread = keep.tile([P, BANK], F32, name="gain_spread")
+        last_bf16 = keep.tile([P, 2 * BANK], BF16, name="last_bf16", align_bytes=64)
         gains = gain_bank.tile([P, PASSES * 2 * PACK], F32, name="gains")
 
         w_raw = [keep.tile([P, H], U32, name="w_raw%d" % a) for a in range(2)]
@@ -125,27 +127,28 @@ def tile_mtgnnantisymmetricgraphlearner_w8_kernel(
             for j in range(n):
                 e_mx[pair, a0 + j] = (codes[:, j * PAIR : (j + 1) * PAIR], scale[:, j * PAIR : (j + 1) * PAIR])
 
-        def project(pair, a, g, u):
+        def project(pair, a, g, j):
             codes, scale = e_mx[pair, a]
             bank = banks.tile([P, BANK], F32, name="bank")
-            for e in range(2):
-                t = 2 * u + e
+            for t in range(PACK):
                 nc.tensor.matmul_mx(
-                    out=bank[:, e * PAIR : (e + 1) * PAIR],
+                    out=bank[:, t * P : (t + 1) * P],
                     lhsT=w_codes[a][g][:, t * P : (t + 1) * P].bitcast(FP8X4),
                     lhsT_scale=w_scale[a][:, g * BANK + t * P : g * BANK + (t + 1) * P],
-                    rhs=codes.bitcast(FP8X4),
-                    rhs_scale=scale,
+                    rhs=codes[:, j * P : (j + 1) * P].bitcast(FP8X4),
+                    rhs_scale=scale[:, j * P : (j + 1) * P],
                     start=True,
                     stop=True,
                 )
-            proj[pair, a, g, u] = bank
+            proj[pair, a, g, j] = bank
 
-        def tanh_proj(pair, a, g, u):
-            if u == 0:
-                tanh_vals[pair, a, g] = tanh_pool.tile([P, 2, PAIR, 2], F32, name="tanh_vals")
+        def tanh_proj(pair, a, g, j):
+            if j == 0:
+                tanh_vals[pair, a, g] = tanh_pool.tile([P, 2 * BANK], F32, name="tanh_vals")
             nc.scalar.activation(
-                out=tanh_vals[pair, a, g][:, u, :, :], in_=proj[pair, a, g, u][:].rearrange("p (e n) -> p n e", e=2), func=ACT.Tanh
+                out=tanh_vals[pair, a, g][:, j * BANK : (j + 1) * BANK].rearrange("p (n t) -> p n t", t=PACK),
+                in_=proj[pair, a, g, j][:].rearrange("p (t n) -> p n t", t=PACK),
+                func=ACT.Tanh,
             )
 
         def project_side(pair, a):
@@ -156,26 +159,43 @@ def tile_mtgnnantisymmetricgraphlearner_w8_kernel(
                 for u in range(2):
                     tanh_proj(pair, a, g, u)
 
-        def apply_gain(c, n, a, g):
-            pair, lo = c // 2, (c % 2) * P
-            if g == 0:
-                m_bf16[c, a] = work.tile([P, PASSES * PAIR * PACK], BF16, name="m_bf16_%d" % a, align_bytes=64)
+        def gain_tile(c, n, a, g):
+            if (a, g) == (1, 1):
+                m_bf16[c, a, g] = last_bf16[:, 0 : n * BANK]
+            elif a == 1:
+                m_bf16[c, a, g] = work.tile([P, 2 * BANK], BF16, name="m2_bf16", align_bytes=64)[:, 0 : n * BANK]
+            elif g == 0:
+                both = work.tile([P, PASSES * 2 * BANK], BF16, name="m1_bf16", align_bytes=64)
+                m_bf16[c, a] = both
+                for h in range(PASSES):
+                    m_bf16[c, a, h] = both[:, h * n * BANK : (h + 1) * n * BANK]
+            return m_bf16[c, a, g]
+
+        def apply_gain(c, n, a, g, lo=0):
+            start = (c % 2) * BANK
             col = (2 * g + a) * PACK
-            width = n * P * PACK
             nc.vector.tensor_tensor(
-                out=m_bf16[c, a][:, g * width : (g + 1) * width].rearrange("p (n u e) -> p n u e", u=2, e=2),
-                in0=tanh_vals[pair, a, g][:, :, lo : lo + n * P, :].rearrange("p u n e -> p n u e"),
-                in1=gains[:, col : col + PACK].rearrange("p (u e) -> p u e", e=2).unsqueeze(1).to_broadcast([P, n * P, 2, 2]),
+                out=gain_tile(c, n, a, g)[:, lo:].rearrange("p (n t) -> p n t", t=PACK),
+                in0=tanh_vals[c // 2, a, g][:, start + lo : start + n * BANK].rearrange("p (n t) -> p n t", t=PACK),
+                in1=gains[:, col : col + PACK].unsqueeze(1).to_broadcast([P, n * P - lo // PACK, PACK]),
+                op=ALU.mult,
+            )
+
+        def apply_gain_pool(c, n, hi):
+            start = (c % 2) * BANK
+            nc.gpsimd.tensor_tensor(
+                out=gain_tile(c, n, 1, 1)[:, 0:hi].rearrange("p (j x) -> p j x", j=n),
+                in0=tanh_vals[c // 2, 1, 1][:, start : start + hi].rearrange("p (j x) -> p j x", j=n),
+                in1=gain_spread[:, 0 : hi // n].unsqueeze(1).to_broadcast([P, n, hi // n]),
                 op=ALU.mult,
             )
 
         def quantize_m(c, n, a, g):
             nodes = slice(c * P, (c + n) * P)
-            width = n * P * PACK
             nc.vector.quantize_mx(
                 out=m_codes[a][g][:, nodes].bitcast(FP8X4),
                 scales=m_scale[a][g][:, nodes],
-                in_=m_bf16[c, a][:, g * width : (g + 1) * width],
+                in_=m_bf16[c, a, g],
             )
 
         def negate_m1(c, n):
@@ -286,16 +306,22 @@ def tile_mtgnnantisymmetricgraphlearner_w8_kernel(
             quantize_m(c, n, 1, 0)
             quantize_m(c, n, 1, 1)
 
-        def finish_nodes(c, n):
+        def finish_nodes(c, n, share, lower=None, e_pair=None):
+            apply_gain_pool(c, n, share)
             apply_gain(c, n, 0, 0)
             apply_gain(c, n, 0, 1)
             apply_gain(c, n, 1, 0)
+            if share < n * BANK:
+                apply_gain(c, n, 1, 1, share)
+            if e_pair is not None:
+                quantize_e(e_pair, 0, 2)
             negate_m1(c, n)
             quantize_m(c, n, 0, 0)
             quantize_m(c, n, 0, 1)
-            apply_gain(c, n, 1, 1)
             quantize_neg(c, n)
             quantize_m(c, n, 1, 0)
+            if lower is not None:
+                store_lower(lower, 0, (lower + 1) * P, on_vector=True)
             quantize_m(c, n, 1, 1)
 
         def mirror_row(c):
@@ -375,12 +401,19 @@ def tile_mtgnnantisymmetricgraphlearner_w8_kernel(
                 start=True,
                 stop=True,
             )
+        last_gain = banks.tile([P, BANK], F32, name="bank")
+        nc.tensor.matmul(last_gain[:, 0:PACK], lhsT=gain_rows[:, P : 2 * P], rhs=pick_rows[:, PACK : 2 * PACK], start=True, stop=True)
         turn_e(0, 1)
         turn_e(1, 0)
-        turn_e(1, 1)
         for g in range(PASSES):
             for u in range(2):
                 tanh_proj(0, 0, g, u)
+        turn_e(1, 1)
+        nc.scalar.activation(
+            out=gain_spread[:].rearrange("p (n t) -> p n t", t=PACK),
+            in_=last_gain[:, 0:PACK].unsqueeze(1).to_broadcast([P, P, PACK]),
+            func=ACT.Copy,
+        )
         group_e(0, 1)
         group_e(1, 0)
         group_e(1, 1)
@@ -416,53 +449,31 @@ def tile_mtgnnantisymmetricgraphlearner_w8_kernel(
         project_side(2, 0)
         score_row(0)
         score_row(1)
-        apply_gain(2, 2, 0, 0)
-        apply_gain(2, 2, 0, 1)
-        quantize_e(3, 0, 2)
-        negate_m1(2, 2)
-        quantize_m(2, 2, 0, 0)
-        quantize_m(2, 2, 0, 1)
+        finish_nodes(2, 2, 768, e_pair=3)
         project_side(2, 1)
         mirror_pair(0)
         store_lower(0, 0, P, on_vector=False)
         store_lower(1, 0, 2 * P, on_vector=False)
         project_side(3, 0)
-        side_two(2, 2)
         score_row(2)
         score_row(3)
         project_side(3, 1)
         last = CHUNKS - 1
-        finish_nodes(4, 1)
+        finish_nodes(4, 1, 384)
         mirror_pair(1)
         store_lower(2, 0, 3 * P, on_vector=False)
-        store_lower(3, 0, 4 * P, on_vector=False)
+        finish_nodes(5, 1, 384, 3)
         score_row(4)
-        store_lower(4, 0, 5 * P, on_vector=False)
-        finish_nodes(5, 1)
         score_row(5)
         mirror_row(4)
+        finish_nodes(6, 1, 384, 4)
         store_lower(5, 0, 6 * P, on_vector=False)
         mirror_row(5)
-        finish_nodes(6, 1)
         score_row(6)
-        store_lower(6, 0, 7 * P, on_vector=False)
+        finish_nodes(7, 1, 384)
+        store_lower(6, 0, 7 * P, on_vector=True)
         mirror_row(6)
-        apply_gain(last, 1, 0, 0)
-        apply_gain(last, 1, 0, 1)
-        apply_gain(last, 1, 1, 0)
-        negate_m1(last, 1)
-        quantize_m(last, 1, 0, 0)
-        quantize_m(last, 1, 0, 1)
-        quantize_neg(last, 1)
-        quantize_m(last, 1, 1, 0)
-        apply_gain(last, 1, 1, 1)
-        quantize_m(last, 1, 1, 1)
-        for c0, width in spans(last):
-            score[last, c0] = banks.tile([P, BANK], F32, name="bank")
-        for c0, step in [(0, 0), (0, 1), (0, 2), (BANK, 0), (BANK, 2), (0, 3), (BANK, 1), (BANK, 3)]:
-            score_pass(last, score[last, c0][:], slice(c0, c0 + BANK), step, step == 0, step == 3)
-        for c0, width in spans(last):
-            tanh_span(last, c0, width)
+        score_row(last)
         for i0, n in mirror_spans(last):
             turn_t(last, i0, n)
         store_lower(last, 0, BANK, on_vector=True)

@@ -20,10 +20,10 @@ P = 128
 PACK = 4
 RUN = 8
 BANK = 512
-CHUNKS = N // P
 PAIR = 2 * P
-PAIRS = CHUNKS // 2
+CHUNKS = N // P
 PASSES = H // (P * PACK)
+SIDES = 2
 SCORE_SCALE = -1.5 / 32.0
 
 
@@ -34,66 +34,70 @@ def tile_mtgnnantisymmetricgraphlearner_w8_kernel(
     with ExitStack() as ctx:
         keep = ctx.enter_context(tc.tile_pool(name="keep", bufs=1))
         work = ctx.enter_context(tc.tile_pool(name="work", bufs=3))
-        results = ctx.enter_context(tc.tile_pool(name="results", bufs=4))
+        results = ctx.enter_context(tc.tile_pool(name="results", bufs=5))
         tanh_pool = ctx.enter_context(tc.tile_pool(name="tanh", bufs=10))
         banks = ctx.enter_context(tc.psum_pool(name="banks", bufs=7))
         gain_bank = ctx.enter_context(tc.psum_pool(name="gain_bank", bufs=1))
         ctx.enter_context(tc.manual_schedule())
 
-        ident_f32 = keep.tile([P, P], F32, name="ident_f32")
-        pick_rows = keep.tile([P, 2 * PACK], BF16, name="pick_rows")
+        ident = keep.tile([P, P], F32, name="ident")
+        pick_rows = keep.tile([P, SIDES * PACK], BF16, name="pick_rows")
         gain_rows = keep.tile([P, PASSES * P], BF16, name="gain_rows")
         scale_cols = keep.tile([P, PACK], F32, name="scale_cols")
         scale_spread = keep.tile([P, 2 * D], F32, name="scale_spread")
         gain_spread = keep.tile([P, BANK], F32, name="gain_spread")
-        last_bf16 = keep.tile([P, 2 * BANK], BF16, name="last_bf16", align_bytes=64)
-        gains = gain_bank.tile([P, PASSES * 2 * PACK], F32, name="gains")
+        m2_last = keep.tile([P, 2 * BANK], BF16, name="m2_last", align_bytes=64)
+        gains = gain_bank.tile([P, PASSES * SIDES * PACK], F32, name="gains")
 
-        w_raw = [keep.tile([P, H], U32, name="w_raw%d" % a) for a in range(2)]
-        ws_raw = [keep.tile([P, H], U8, name="ws_raw%d" % a) for a in range(2)]
-        w_codes = [[keep.tile([P, BANK], U32, name="w_codes%d%d" % (a, g), align_bytes=64) for g in range(PASSES)] for a in range(2)]
-        w_scale = [keep.tile([P, H], U8, name="w_scale%d" % a, align_bytes=64) for a in range(2)]
+        w_raw = [keep.tile([P, H], U32, name="w_raw%d" % s) for s in range(SIDES)]
+        ws_raw = [keep.tile([P, H], U8, name="ws_raw%d" % s) for s in range(SIDES)]
+        w_codes = [[keep.tile([P, BANK], U32, name="w_codes%d%d" % (s, g), align_bytes=64) for g in range(PASSES)] for s in range(SIDES)]
+        w_scale = [keep.tile([P, H], U8, name="w_scale%d" % s, align_bytes=64) for s in range(SIDES)]
 
-        e1_loads = [(0, 2), (2, 2), (4, 4)]
-        e2_loads = [(0, 2), (2, 2), (4, 4)]
-        e1_tiles = [keep.tile([P, n * D], BF16, name="e1_rows%d" % c0) for c0, n in e1_loads]
-        e2_tiles = [keep.tile([P, n * D], U8, name="e2_fp8_rows%d" % c0) for c0, n in e2_loads]
+        e_loads = [(0, 2), (2, 2), (4, 4)]
+        e1_tiles = [keep.tile([P, n * D], BF16, name="e1_rows%d" % c0) for c0, n in e_loads]
+        e2_tiles = [keep.tile([P, n * D], U8, name="e2_fp8_rows%d" % c0) for c0, n in e_loads]
         e_rows = [{}, {}]
         e2_fp8 = {}
-        for (c0, n), t in zip(e1_loads, e1_tiles):
+        for (c0, n), e1_tile, e2_tile in zip(e_loads, e1_tiles, e2_tiles):
             for j in range(0, n, 2):
-                e_rows[0][(c0 + j) // 2] = t[:, j * D : (j + 2) * D]
-        for (c0, n), t in zip(e2_loads, e2_tiles):
-            for j in range(0, n, 2):
-                e2_fp8[(c0 + j) // 2] = t[:, j * D : (j + 2) * D]
+                e_rows[0][(c0 + j) // 2] = e1_tile[:, j * D : (j + 2) * D]
+                e2_fp8[(c0 + j) // 2] = e2_tile[:, j * D : (j + 2) * D]
 
-        m_codes = [[keep.tile([P, N], U32, name="m_codes%d%d" % (a, g), align_bytes=64) for g in range(PASSES)] for a in range(2)]
-        m_scale = [[keep.tile([P, N], U8, name="m_scale%d%d" % (a, g), align_bytes=64) for g in range(PASSES)] for a in range(2)]
+        m_codes = [[keep.tile([P, N], U32, name="m_codes%d%d" % (s, g), align_bytes=64) for g in range(PASSES)] for s in range(SIDES)]
+        m_scale = [[keep.tile([P, N], U8, name="m_scale%d%d" % (s, g), align_bytes=64) for g in range(PASSES)] for s in range(SIDES)]
 
         e_turned, e_grouped, e_mx = {}, {}, {}
-        proj, tanh_vals, m_bf16, neg_bf16, neg_mx = {}, {}, {}, {}, {}
-        score, t_vals, t_turned, row_res = {}, {}, {}, {}
+        proj, tanh_vals, m_bf16, m1_whole, neg_bf16, neg_mx = {}, {}, {}, {}, {}, {}
+        score, t_vals, t_turned = {}, {}, {}
 
-        def load_rows(tile_ap, src, c0, n):
-            nc.sync.dma_start(out=tile_ap[:].rearrange("p (c k) -> p c k", k=D), in_=src[c0 * P : (c0 + n) * P, :].rearrange("(c p) k -> p c k", p=P))
-
-        def load_w_scales(a, src):
-            for q in range(4):
-                nc.sync.dma_start(out=ws_raw[a][32 * q : 32 * q + 4, :].bitcast(I32), in_=src[0, 4 * q : 4 * q + 4, :].bitcast(I32))
-
-        def word_view(src):
-            return src[0].rearrange("p n t -> p (n t)").bitcast(I32)
-
-        def order_w_scales(a):
-            nc.vector.tensor_copy(
-                out=w_scale[a][:].bitcast(I32).rearrange("p (g t b r) -> p g t b r", g=PASSES, t=PACK, r=RUN // 4),
-                in_=ws_raw[a][:].bitcast(I32).rearrange("p (g b t r) -> p g t b r", g=PASSES, t=PACK, r=RUN // 4),
+        def load_rows(dst, src, c0, n):
+            nc.sync.dma_start(
+                out=dst[:].rearrange("p (c k) -> p c k", k=D),
+                in_=src[c0 * P : (c0 + n) * P, :].rearrange("(c p) k -> p c k", p=P),
             )
 
-        def order_w_codes(a, g):
+        def load_w_words(s, src):
+            nc.sync.dma_start(out=w_raw[s][:].bitcast(I32), in_=src[0].rearrange("p n t -> p (n t)").bitcast(I32))
+
+        def load_w_scales(s, src):
+            for q in range(4):
+                nc.sync.dma_start(
+                    out=ws_raw[s][32 * q : 32 * q + 4, :].bitcast(I32),
+                    in_=src[0, 4 * q : 4 * q + 4, :].bitcast(I32),
+                )
+
+        def order_w_scales(s):
+            words = RUN // 4
             nc.vector.tensor_copy(
-                out=w_codes[a][g][:].bitcast(I32).rearrange("p (t b r) -> p t b r", t=PACK, r=RUN),
-                in_=w_raw[a][:, g * BANK : (g + 1) * BANK].bitcast(I32).rearrange("p (b t r) -> p t b r", t=PACK, r=RUN),
+                out=w_scale[s][:].bitcast(I32).rearrange("p (g t b r) -> p g t b r", g=PASSES, t=PACK, r=words),
+                in_=ws_raw[s][:].bitcast(I32).rearrange("p (g b t r) -> p g t b r", g=PASSES, t=PACK, r=words),
+            )
+
+        def order_w_codes(s, g):
+            nc.vector.tensor_copy(
+                out=w_codes[s][g][:].bitcast(I32).rearrange("p (t b r) -> p t b r", t=PACK, r=RUN),
+                in_=w_raw[s][:, g * BANK : (g + 1) * BANK].bitcast(I32).rearrange("p (b t r) -> p t b r", t=PACK, r=RUN),
             )
 
         def scale_e2(pair):
@@ -101,107 +105,121 @@ def tile_mtgnnantisymmetricgraphlearner_w8_kernel(
             nc.vector.tensor_tensor(out=rows[:], in0=e2_fp8[pair].bitcast(FP8), in1=scale_spread[:], op=ALU.mult)
             e_rows[1][pair] = rows[:]
 
-        def turn_e(pair, a):
+        def turn_e(pair, s):
             bank = banks.tile([P, BANK], F32, name="bank")
-            words = e_rows[a][pair].bitcast(F32)
+            twos = e_rows[s][pair].bitcast(F32)
             for j in range(2):
                 for u in range(2):
                     col = (2 * j + u) * P
-                    nc.tensor.transpose(bank[:, col : col + P], words[:, j * 2 * P + u : (j + 1) * 2 * P : 2], ident_f32[:])
-            e_turned[pair, a] = bank
+                    nc.tensor.transpose(bank[:, col : col + P], twos[:, j * 2 * P + u : (j + 1) * 2 * P : 2], ident[:])
+            e_turned[pair, s] = bank
 
-        def group_e(pair, a, on_vector=False):
-            if a == 0:
-                e_grouped[pair] = work.tile([P, 2 * PAIR * PACK], BF16, name="e_grouped", align_bytes=64)
-            dst = e_grouped[pair][:].bitcast(F32)[:, a * BANK : (a + 1) * BANK].rearrange("p (j n u) -> p j n u", n=P, u=2)
-            src = e_turned[pair, a][:].rearrange("p (j u n) -> p j n u", n=P, u=2)
-            if on_vector:
-                nc.vector.tensor_copy(out=dst, in_=src)
-            else:
-                nc.scalar.copy(out=dst, in_=src)
+        def group_e(pair, s):
+            if s == 0:
+                e_grouped[pair] = work.tile([P, SIDES * PAIR * PACK], BF16, name="e_grouped", align_bytes=64)
+            nc.scalar.copy(
+                out=e_grouped[pair][:].bitcast(F32)[:, s * BANK : (s + 1) * BANK].rearrange("p (j n u) -> p j n u", n=P, u=2),
+                in_=e_turned[pair, s][:].rearrange("p (j u n) -> p j n u", n=P, u=2),
+            )
 
-        def quantize_e(pair, a0, n):
-            codes = keep.tile([P, n * PAIR], U32, name="e_codes%d%d" % (pair, a0), align_bytes=64)
-            scale = keep.tile([P, n * PAIR], U8, name="e_scale%d%d" % (pair, a0), align_bytes=64)
-            nc.vector.quantize_mx(out=codes[:].bitcast(FP8X4), scales=scale[:], in_=e_grouped[pair][:, a0 * PAIR * PACK : (a0 + n) * PAIR * PACK])
-            for j in range(n):
-                e_mx[pair, a0 + j] = (codes[:, j * PAIR : (j + 1) * PAIR], scale[:, j * PAIR : (j + 1) * PAIR])
+        def quantize_e(pair, first, sides):
+            codes = keep.tile([P, sides * PAIR], U32, name="e_codes%d%d" % (pair, first), align_bytes=64)
+            scale = keep.tile([P, sides * PAIR], U8, name="e_scale%d%d" % (pair, first), align_bytes=64)
+            nc.vector.quantize_mx(
+                out=codes[:].bitcast(FP8X4),
+                scales=scale[:],
+                in_=e_grouped[pair][:, first * PAIR * PACK : (first + sides) * PAIR * PACK],
+            )
+            for i in range(sides):
+                e_mx[pair, first + i] = (codes[:, i * PAIR : (i + 1) * PAIR], scale[:, i * PAIR : (i + 1) * PAIR])
 
-        def project(pair, a, g, j):
-            codes, scale = e_mx[pair, a]
+        def turn_and_group_e(pair):
+            for s in range(SIDES):
+                turn_e(pair, s)
+            for s in range(SIDES):
+                group_e(pair, s)
+
+        def project(pair, s, g, j):
+            codes, scale = e_mx[pair, s]
             bank = banks.tile([P, BANK], F32, name="bank")
             for t in range(PACK):
                 nc.tensor.matmul_mx(
                     out=bank[:, t * P : (t + 1) * P],
-                    lhsT=w_codes[a][g][:, t * P : (t + 1) * P].bitcast(FP8X4),
-                    lhsT_scale=w_scale[a][:, g * BANK + t * P : g * BANK + (t + 1) * P],
+                    lhsT=w_codes[s][g][:, t * P : (t + 1) * P].bitcast(FP8X4),
+                    lhsT_scale=w_scale[s][:, g * BANK + t * P : g * BANK + (t + 1) * P],
                     rhs=codes[:, j * P : (j + 1) * P].bitcast(FP8X4),
                     rhs_scale=scale[:, j * P : (j + 1) * P],
                     start=True,
                     stop=True,
                 )
-            proj[pair, a, g, j] = bank
+            proj[pair, s, g, j] = bank
 
-        def tanh_proj(pair, a, g, j):
+        def tanh_proj(pair, s, g, j):
             if j == 0:
-                tanh_vals[pair, a, g] = tanh_pool.tile([P, 2 * BANK], F32, name="tanh_vals")
+                tanh_vals[pair, s, g] = tanh_pool.tile([P, 2 * BANK], F32, name="tanh_vals")
             nc.scalar.activation(
-                out=tanh_vals[pair, a, g][:, j * BANK : (j + 1) * BANK].rearrange("p (n t) -> p n t", t=PACK),
-                in_=proj[pair, a, g, j][:].rearrange("p (t n) -> p n t", t=PACK),
+                out=tanh_vals[pair, s, g][:, j * BANK : (j + 1) * BANK].rearrange("p (n t) -> p n t", t=PACK),
+                in_=proj[pair, s, g, j][:].rearrange("p (t n) -> p n t", t=PACK),
                 func=ACT.Tanh,
             )
 
-        def project_side(pair, a):
+        def project_all(pair, s):
             for g in range(PASSES):
-                for u in range(2):
-                    project(pair, a, g, u)
-            for g in range(PASSES):
-                for u in range(2):
-                    tanh_proj(pair, a, g, u)
+                for j in range(2):
+                    project(pair, s, g, j)
 
-        def gain_tile(c, n, a, g):
-            if (a, g) == (1, 1):
-                m_bf16[c, a, g] = last_bf16[:, 0 : n * BANK]
-            elif a == 1:
-                m_bf16[c, a, g] = work.tile([P, 2 * BANK], BF16, name="m2_bf16", align_bytes=64)[:, 0 : n * BANK]
+        def tanh_all(pair, s):
+            for g in range(PASSES):
+                for j in range(2):
+                    tanh_proj(pair, s, g, j)
+
+        def project_side(pair, s):
+            project_all(pair, s)
+            tanh_all(pair, s)
+
+        def m_tile(c, n, s, g):
+            if s == 1 and g == PASSES - 1:
+                m_bf16[c, s, g] = m2_last[:, 0 : n * BANK]
+            elif s == 1:
+                m2_first = work.tile([P, 2 * BANK], BF16, name="m2_first", align_bytes=64)
+                m_bf16[c, s, g] = m2_first[:, 0 : n * BANK]
             elif g == 0:
-                both = work.tile([P, PASSES * 2 * BANK], BF16, name="m1_bf16", align_bytes=64)
-                m_bf16[c, a] = both
-                for h in range(PASSES):
-                    m_bf16[c, a, h] = both[:, h * n * BANK : (h + 1) * n * BANK]
-            return m_bf16[c, a, g]
+                m1_whole[c] = work.tile([P, PASSES * 2 * BANK], BF16, name="m1_whole", align_bytes=64)
+                for i in range(PASSES):
+                    m_bf16[c, s, i] = m1_whole[c][:, i * n * BANK : (i + 1) * n * BANK]
+            return m_bf16[c, s, g]
 
-        def apply_gain(c, n, a, g, lo=0):
+        def apply_gain(c, n, s, g, done):
             start = (c % 2) * BANK
-            col = (2 * g + a) * PACK
+            cols = (n - done) * BANK
+            col = (SIDES * g + s) * PACK
             nc.vector.tensor_tensor(
-                out=gain_tile(c, n, a, g)[:, lo:].rearrange("p (n t) -> p n t", t=PACK),
-                in0=tanh_vals[c // 2, a, g][:, start + lo : start + n * BANK].rearrange("p (n t) -> p n t", t=PACK),
-                in1=gains[:, col : col + PACK].unsqueeze(1).to_broadcast([P, n * P - lo // PACK, PACK]),
+                out=m_tile(c, n, s, g)[:, 0:cols].rearrange("p (n t) -> p n t", t=PACK),
+                in0=tanh_vals[c // 2, s, g][:, start : start + cols].rearrange("p (n t) -> p n t", t=PACK),
+                in1=gains[:, col : col + PACK].unsqueeze(1).to_broadcast([P, cols // PACK, PACK]),
                 op=ALU.mult,
             )
 
-        def apply_gain_pool(c, n, hi):
-            start = (c % 2) * BANK
+        def apply_last_gain_on_gpsimd(c, n, taken):
+            end = (c % 2 + n) * BANK
+            cols = taken * BANK
             nc.gpsimd.tensor_tensor(
-                out=gain_tile(c, n, 1, 1)[:, 0:hi].rearrange("p (j x) -> p j x", j=n),
-                in0=tanh_vals[c // 2, 1, 1][:, start : start + hi].rearrange("p (j x) -> p j x", j=n),
-                in1=gain_spread[:, 0 : hi // n].unsqueeze(1).to_broadcast([P, n, hi // n]),
+                out=m_tile(c, n, 1, PASSES - 1)[:, n * BANK - cols : n * BANK].rearrange("p (j x) -> p j x", j=taken),
+                in0=tanh_vals[c // 2, 1, PASSES - 1][:, end - cols : end].rearrange("p (j x) -> p j x", j=taken),
+                in1=gain_spread[:].unsqueeze(1).to_broadcast([P, taken, BANK]),
                 op=ALU.mult,
             )
 
-        def quantize_m(c, n, a, g):
+        def quantize_m(c, n, s, g):
             nodes = slice(c * P, (c + n) * P)
             nc.vector.quantize_mx(
-                out=m_codes[a][g][:, nodes].bitcast(FP8X4),
-                scales=m_scale[a][g][:, nodes],
-                in_=m_bf16[c, a, g],
+                out=m_codes[s][g][:, nodes].bitcast(FP8X4), scales=m_scale[s][g][:, nodes], in_=m_bf16[c, s, g]
             )
 
         def negate_m1(c, n):
-            width = PASSES * n * P * PACK
-            neg = work.tile([P, PASSES * PAIR * PACK], BF16, name="neg_bf16", align_bytes=64)
-            nc.vector.tensor_scalar(out=neg[:, 0:width], in0=m_bf16[c, 0][:, 0:width], scalar1=-1.0, scalar2=None, op0=ALU.mult)
+            width = PASSES * n * BANK
+            neg = work.tile([P, PASSES * 2 * BANK], BF16, name="neg_bf16", align_bytes=64)
+            nc.vector.tensor_scalar(out=neg[:, 0:width], in0=m1_whole[c][:, 0:width], scalar1=-1.0, scalar2=None, op0=ALU.mult)
             neg_bf16[c] = neg
 
         def quantize_neg(c, n):
@@ -214,34 +232,44 @@ def tile_mtgnnantisymmetricgraphlearner_w8_kernel(
                     cols = slice((g * n + j) * P, (g * n + j + 1) * P)
                     neg_mx[c + j, g] = (codes[:, cols], scale[:, cols])
 
+        def gain_products(c, n):
+            apply_last_gain_on_gpsimd(c, n, n)
+            apply_gain(c, n, 0, 0, 0)
+            apply_gain(c, n, 0, 1, 0)
+            apply_gain(c, n, 1, 0, 0)
+
+        def quantize_all_but_last(c, n):
+            negate_m1(c, n)
+            quantize_m(c, n, 0, 0)
+            quantize_m(c, n, 0, 1)
+            quantize_neg(c, n)
+            quantize_m(c, n, 1, 0)
+
+        def quantize_last(c, n):
+            quantize_m(c, n, 1, PASSES - 1)
+
         def spans(c):
             width = (c + 1) * P
             return [(c0, min(BANK, width - c0)) for c0 in range(0, width, BANK)]
 
-        def score_pass(c, bank_cols, cols, step, start, stop):
-            g = step % PASSES
-            if step < PASSES:
-                lhs, lhs_scale = neg_mx[c, g]
-                a = 1
-            else:
-                lhs, lhs_scale = m_codes[1][g][:, c * P : (c + 1) * P], m_scale[1][g][:, c * P : (c + 1) * P]
-                a = 0
-            nc.tensor.matmul_mx(
-                out=bank_cols,
-                lhsT=lhs.bitcast(FP8X4),
-                lhsT_scale=lhs_scale,
-                rhs=m_codes[a][g][:, cols].bitcast(FP8X4),
-                rhs_scale=m_scale[a][g][:, cols],
-                start=start,
-                stop=stop,
-            )
-
         def score_span(c, c0, width):
             bank = banks.tile([P, BANK], F32, name="bank")
-            groups = [(0, 2 * P), (2 * P, P)] if width == 3 * P else [(0, width)]
+            nodes = slice(c * P, (c + 1) * P)
+            steps = [neg_mx[c, g] + (1, g) for g in range(PASSES)]
+            steps = steps + [(m_codes[1][g][:, nodes], m_scale[1][g][:, nodes], 0, g) for g in range(PASSES)]
+            groups = [(0, PAIR), (PAIR, P)] if width == PAIR + P else [(0, width)]
             for off, n in groups:
-                for step in range(2 * PASSES):
-                    score_pass(c, bank[:, off : off + n], slice(c0 + off, c0 + off + n), step, step == 0, step == 2 * PASSES - 1)
+                cols = slice(c0 + off, c0 + off + n)
+                for i, (lhs, lhs_scale, s, g) in enumerate(steps):
+                    nc.tensor.matmul_mx(
+                        out=bank[:, off : off + n],
+                        lhsT=lhs.bitcast(FP8X4),
+                        lhsT_scale=lhs_scale,
+                        rhs=m_codes[s][g][:, cols].bitcast(FP8X4),
+                        rhs_scale=m_scale[s][g][:, cols],
+                        start=(i == 0),
+                        stop=(i == len(steps) - 1),
+                    )
             score[c, c0] = bank
 
         def tanh_span(c, c0, width):
@@ -249,25 +277,50 @@ def tile_mtgnnantisymmetricgraphlearner_w8_kernel(
                 t_vals[c] = results.tile([P, N], F32, name="t_vals")
             nc.scalar.activation(out=t_vals[c][:, c0 : c0 + width], in_=score[c, c0][:, 0:width], func=ACT.Tanh, scale=SCORE_SCALE)
 
-        def store_lower(c, c0, width, on_vector):
-            res = results.tile([P, N], F32, name="lower")
-            if on_vector:
-                nc.vector.tensor_scalar(out=res[:, 0:width], in0=t_vals[c][:, c0 : c0 + width], scalar1=0.0, scalar2=None, op0=ALU.max)
-            else:
-                nc.scalar.activation(out=res[:, 0:width], in_=t_vals[c][:, c0 : c0 + width], func=ACT.Relu)
-            nc.sync.dma_start(out=out[c * P : (c + 1) * P, c0 : c0 + width], in_=res[:, 0:width])
-
         def score_row(c):
             for c0, width in spans(c):
                 score_span(c, c0, width)
             for c0, width in spans(c):
                 tanh_span(c, c0, width)
 
-        def relu_neg(dst, src, on_vector):
+        def store_lower(c, c0, width, on_vector):
+            res = results.tile([P, N], F32, name="lower")
+            src = t_vals[c][:, c0 : c0 + width]
+            if on_vector:
+                nc.vector.tensor_scalar(out=res[:, 0:width], in0=src, scalar1=0.0, scalar2=None, op0=ALU.max)
+            else:
+                nc.scalar.activation(out=res[:, 0:width], in_=src, func=ACT.Relu)
+            nc.sync.dma_start(out=out[c * P : (c + 1) * P, c0 : c0 + width], in_=res[:, 0:width])
+
+        def store_lower_row(c, on_vector):
+            store_lower(c, 0, (c + 1) * P, on_vector)
+
+        def relu_of_negative(dst, src, on_vector):
             if on_vector:
                 nc.vector.tensor_scalar(out=dst, in0=src, scalar1=-1.0, scalar2=0.0, op0=ALU.mult, op1=ALU.max)
             else:
                 nc.scalar.activation(out=dst, in_=src, func=ACT.Relu, scale=-1.0)
+
+        def turn_t(c, i0, n):
+            bank = banks.tile([P, BANK], F32, name="bank")
+            for i in range(n):
+                nc.tensor.transpose(bank[:, i * P : (i + 1) * P], t_vals[c][:, (i0 + i) * P : (i0 + i + 1) * P], ident[:])
+            t_turned[c, i0] = bank
+
+        def store_upper(c, i0, n, on_vector):
+            res = results.tile([P, BANK], F32, name="upper")
+            relu_of_negative(res[:, 0 : n * P], t_turned[c, i0][:, 0 : n * P], on_vector)
+            nc.sync.dma_start(
+                out=out[i0 * P : (i0 + n) * P, c * P : (c + 1) * P].rearrange("(i p) n -> p i n", p=P),
+                in_=res[:, 0 : n * P].rearrange("p (i n) -> p i n", n=P),
+            )
+
+        def mirror_row(c):
+            blocks = [(i0, min(BANK // P, c - i0)) for i0 in range(0, c, BANK // P)]
+            for i0, n in blocks:
+                turn_t(c, i0, n)
+            for i0, n in blocks:
+                store_upper(c, i0, n, on_vector=False)
 
         def mirror_pair(pair):
             c = 2 * pair
@@ -277,206 +330,164 @@ def tile_mtgnnantisymmetricgraphlearner_w8_kernel(
                 for i in range(2):
                     for j in range(2):
                         col = (2 * i + j) * P
-                        nc.tensor.transpose(bank[:, col : col + P], t_vals[c + j][:, (i0 + i) * P : (i0 + i + 1) * P], ident_f32[:])
+                        nc.tensor.transpose(bank[:, col : col + P], t_vals[c + j][:, (i0 + i) * P : (i0 + i + 1) * P], ident[:])
                 turned.append((i0, bank))
-            inner = banks.tile([P, BANK], F32, name="bank")
-            nc.tensor.transpose(inner[:, 0:P], t_vals[c + 1][:, c * P : (c + 1) * P], ident_f32[:])
+            turn_t(c + 1, c, 1)
             for i0, bank in turned:
                 res = results.tile([P, BANK], F32, name="upper")
-                relu_neg(res[:], bank[:], False)
+                relu_of_negative(res[:], bank[:], on_vector=False)
                 nc.sync.dma_start(
                     out=out[i0 * P : (i0 + 2) * P, c * P : (c + 2) * P].rearrange("(i p) n -> p i n", p=P),
                     in_=res[:].rearrange("p (i n) -> p i n", n=PAIR),
                 )
-            res = results.tile([P, BANK], F32, name="upper")
-            relu_neg(res[:, 0:P], inner[:, 0:P], False)
-            nc.sync.dma_start(out=out[c * P : (c + 1) * P, (c + 1) * P : (c + 2) * P], in_=res[:, 0:P])
+            store_upper(c + 1, c, 1, on_vector=False)
 
-        def side_one(c, n):
-            apply_gain(c, n, 0, 0)
-            apply_gain(c, n, 0, 1)
-            quantize_m(c, n, 0, 0)
-            negate_m1(c, n)
-            quantize_m(c, n, 0, 1)
-
-        def side_two(c, n):
-            apply_gain(c, n, 1, 0)
-            quantize_neg(c, n)
-            apply_gain(c, n, 1, 1)
-            quantize_m(c, n, 1, 0)
-            quantize_m(c, n, 1, 1)
-
-        def finish_nodes(c, n, share, lower=None, e_pair=None):
-            apply_gain_pool(c, n, share)
-            apply_gain(c, n, 0, 0)
-            apply_gain(c, n, 0, 1)
-            apply_gain(c, n, 1, 0)
-            if share < n * BANK:
-                apply_gain(c, n, 1, 1, share)
-            if e_pair is not None:
-                quantize_e(e_pair, 0, 2)
-            negate_m1(c, n)
-            quantize_m(c, n, 0, 0)
-            quantize_m(c, n, 0, 1)
-            quantize_neg(c, n)
-            quantize_m(c, n, 1, 0)
-            if lower is not None:
-                store_lower(lower, 0, (lower + 1) * P, on_vector=True)
-            quantize_m(c, n, 1, 1)
-
-        def mirror_row(c):
-            for i0, n in mirror_spans(c):
-                turn_t(c, i0, n)
-            for i0, n in mirror_spans(c):
-                store_upper(c, i0, n, on_vector=False)
-
-        def mirror_spans(c):
-            return [(i0, min(4, c - i0)) for i0 in range(0, c, 4)]
-
-        def turn_t(c, i0, n):
-            bank = banks.tile([P, BANK], F32, name="bank")
-            for i in range(n):
-                nc.tensor.transpose(bank[:, i * P : (i + 1) * P], t_vals[c][:, (i0 + i) * P : (i0 + i + 1) * P], ident_f32[:])
-            t_turned[c, i0] = bank
-
-        def store_upper(c, i0, n, on_vector):
-            res = results.tile([P, BANK], F32, name="upper")
-            src = t_turned[c, i0][:, 0 : n * P]
-            if on_vector:
-                nc.vector.tensor_scalar(out=res[:, 0 : n * P], in0=src, scalar1=-1.0, scalar2=0.0, op0=ALU.mult, op1=ALU.max)
-            else:
-                nc.scalar.activation(out=res[:, 0 : n * P], in_=src, func=ACT.Relu, scale=-1.0)
-            nc.sync.dma_start(
-                out=out[i0 * P : (i0 + n) * P, c * P : (c + 1) * P].rearrange("(i p) n -> p i n", p=P),
-                in_=res[:, 0 : n * P].rearrange("p (i n) -> p i n", n=P),
-            )
-
-        make_identity(nc, ident_f32[:])
+        make_identity(nc, ident[:])
         nc.vector.memset(ws_raw[0][:].bitcast(I32), 0)
         nc.vector.memset(gain_rows[:], 0.0)
         nc.vector.memset(ws_raw[1][:].bitcast(I32), 0)
-        for a, gain in enumerate((g1, g2)):
+        for s, gain in enumerate((g1, g2)):
             nc.gpsimd.dma_start(
-                out=gain_rows[a * PACK : (a + 1) * PACK, :].rearrange("t (q r) -> t q r", r=RUN),
+                out=gain_rows[s * PACK : (s + 1) * PACK, :].rearrange("t (q r) -> t q r", r=RUN),
                 in_=gain.rearrange("(q t r) -> t q r", t=PACK, r=RUN),
             )
-        nc.vector.tensor_copy(out=pick_rows[:], in_=ident_f32[:, 0 : 2 * PACK])
+        nc.vector.tensor_copy(out=pick_rows[:], in_=ident[:, 0 : SIDES * PACK])
 
-        nc.sync.dma_start(out=scale_cols[:], in_=e2_scale.rearrange("o (n m) -> n (o m)", m=PACK))
-        load_rows(e1_tiles[0], e1, *e1_loads[0])
-        nc.sync.dma_start(out=w_raw[0][:].bitcast(I32), in_=word_view(w1_words))
+        nc.sync.dma_start(out=scale_cols[:], in_=e2_scale.rearrange("o (n t) -> n (o t)", t=PACK))
+        load_rows(e1_tiles[0], e1, *e_loads[0])
+        load_rows(e1_tiles[1], e1, *e_loads[1])
+        load_w_words(0, w1_words)
         load_w_scales(0, w1_scales)
-        load_rows(e2_tiles[0], e2_bytes, *e2_loads[0])
-        load_rows(e1_tiles[1], e1, *e1_loads[1])
-        load_rows(e2_tiles[1], e2_bytes, *e2_loads[1])
-        nc.sync.dma_start(out=w_raw[1][:].bitcast(I32), in_=word_view(w2_words))
+        load_rows(e2_tiles[0], e2_bytes, *e_loads[0])
+        load_rows(e2_tiles[1], e2_bytes, *e_loads[1])
+        load_w_words(1, w2_words)
         load_w_scales(1, w2_scales)
-        load_rows(e2_tiles[2], e2_bytes, *e2_loads[2])
-        load_rows(e1_tiles[2], e1, *e1_loads[2])
+        load_rows(e2_tiles[2], e2_bytes, *e_loads[2])
+        load_rows(e1_tiles[2], e1, *e_loads[2])
 
         spread_bank = banks.tile([P, BANK], F32, name="bank")
         for t in range(PACK):
-            nc.tensor.transpose(spread_bank[:, t * P : (t + 1) * P], scale_cols[:, t : t + 1].to_broadcast([P, P]), ident_f32[:])
+            nc.tensor.transpose(spread_bank[:, t * P : (t + 1) * P], scale_cols[:, t : t + 1].to_broadcast([P, P]), ident[:])
         nc.scalar.activation(
             out=scale_spread[:].rearrange("p (j n t) -> p j n t", j=2, t=PACK),
             in_=spread_bank[:].rearrange("p (t n) -> p n t", t=PACK).unsqueeze(1).to_broadcast([P, 2, P, PACK]),
             func=ACT.Copy,
         )
+
         turn_e(0, 0)
         group_e(0, 0)
+        turn_e(1, 0)
+        group_e(1, 0)
         order_w_codes(0, 0)
-        order_w_codes(0, 1)
-        order_w_scales(0)
         quantize_e(0, 0, 1)
+        order_w_scales(0)
+        order_w_codes(0, 1)
         scale_e2(0)
+        quantize_e(1, 0, 1)
         scale_e2(1)
-        for g in range(PASSES):
-            for u in range(2):
-                project(0, 0, g, u)
+        project_all(0, 0)
         for g in range(PASSES):
             nc.tensor.matmul(
-                gains[:, g * 2 * PACK : (g + 1) * 2 * PACK],
+                gains[:, g * SIDES * PACK : (g + 1) * SIDES * PACK],
                 lhsT=gain_rows[:, g * P : (g + 1) * P],
                 rhs=pick_rows[:],
                 start=True,
                 stop=True,
             )
         last_gain = banks.tile([P, BANK], F32, name="bank")
-        nc.tensor.matmul(last_gain[:, 0:PACK], lhsT=gain_rows[:, P : 2 * P], rhs=pick_rows[:, PACK : 2 * PACK], start=True, stop=True)
+        nc.tensor.matmul(
+            last_gain[:, 0:PACK], lhsT=gain_rows[:, (PASSES - 1) * P : PASSES * P], rhs=pick_rows[:, PACK : 2 * PACK], start=True, stop=True
+        )
         turn_e(0, 1)
-        turn_e(1, 0)
-        for g in range(PASSES):
-            for u in range(2):
-                tanh_proj(0, 0, g, u)
-        turn_e(1, 1)
+        tanh_all(0, 0)
         nc.scalar.activation(
             out=gain_spread[:].rearrange("p (n t) -> p n t", t=PACK),
             in_=last_gain[:, 0:PACK].unsqueeze(1).to_broadcast([P, P, PACK]),
             func=ACT.Copy,
         )
         group_e(0, 1)
-        group_e(1, 0)
+        project_side(1, 0)
+        turn_e(1, 1)
         group_e(1, 1)
+
         order_w_codes(1, 0)
         order_w_codes(1, 1)
         order_w_scales(1)
-        apply_gain(0, 2, 0, 0)
+        apply_gain(0, 2, 0, 0, 0)
         quantize_e(0, 1, 1)
-        apply_gain(0, 2, 0, 1)
-        quantize_e(1, 0, 2)
+        apply_gain(0, 2, 0, 1, 0)
         scale_e2(2)
         negate_m1(0, 2)
         quantize_m(0, 2, 0, 0)
         quantize_m(0, 2, 0, 1)
+        quantize_e(1, 1, 1)
         project_side(0, 1)
-        project_side(1, 0)
-        turn_e(2, 0)
-        turn_e(2, 1)
-        group_e(2, 0)
-        group_e(2, 1)
+        turn_and_group_e(2)
         scale_e2(3)
-        apply_gain(0, 2, 1, 0)
+        apply_last_gain_on_gpsimd(0, 2, 1)
+        apply_gain(0, 2, 1, 0, 0)
+        apply_gain(0, 2, 1, 1, 1)
         quantize_neg(0, 2)
-        apply_gain(0, 2, 1, 1)
-        quantize_e(2, 0, 2)
+        quantize_e(2, 0, SIDES)
         quantize_m(0, 2, 1, 0)
-        quantize_m(0, 2, 1, 1)
+        quantize_last(0, 2)
         project_side(1, 1)
-        turn_e(3, 0)
-        turn_e(3, 1)
-        group_e(3, 0)
-        group_e(3, 1)
+        turn_and_group_e(3)
         project_side(2, 0)
         score_row(0)
         score_row(1)
-        finish_nodes(2, 2, 768, e_pair=3)
+
+        gain_products(2, 2)
+        quantize_e(3, 0, SIDES)
+        quantize_all_but_last(2, 2)
+        quantize_last(2, 2)
         project_side(2, 1)
         mirror_pair(0)
-        store_lower(0, 0, P, on_vector=False)
-        store_lower(1, 0, 2 * P, on_vector=False)
+        store_lower_row(0, on_vector=False)
+        store_lower_row(1, on_vector=False)
         project_side(3, 0)
         score_row(2)
         score_row(3)
         project_side(3, 1)
-        last = CHUNKS - 1
-        finish_nodes(4, 1, 384)
+
+        gain_products(4, 1)
+        quantize_all_but_last(4, 1)
+        quantize_last(4, 1)
         mirror_pair(1)
-        store_lower(2, 0, 3 * P, on_vector=False)
-        finish_nodes(5, 1, 384, 3)
+        store_lower_row(2, on_vector=False)
+
+        gain_products(5, 1)
+        quantize_all_but_last(5, 1)
+        store_lower_row(3, on_vector=True)
+        quantize_last(5, 1)
         score_row(4)
         score_row(5)
         mirror_row(4)
-        finish_nodes(6, 1, 384, 4)
-        store_lower(5, 0, 6 * P, on_vector=False)
+
+        gain_products(6, 1)
+        quantize_all_but_last(6, 1)
+        store_lower_row(4, on_vector=True)
+        quantize_last(6, 1)
+        store_lower_row(5, on_vector=False)
         mirror_row(5)
         score_row(6)
-        finish_nodes(7, 1, 384)
-        store_lower(6, 0, 7 * P, on_vector=True)
-        mirror_row(6)
-        score_row(last)
-        for i0, n in mirror_spans(last):
+
+        last = CHUNKS - 1
+        gain_products(last, 1)
+        quantize_all_but_last(last, 1)
+        quantize_last(last, 1)
+        store_lower_row(last - 1, on_vector=True)
+        mirror_row(last - 1)
+
+        quarters = range(0, N, PAIR)
+        for c0 in quarters:
+            score_span(last, c0, PAIR)
+        for c0 in quarters:
+            tanh_span(last, c0, PAIR)
+        for c0 in quarters:
+            store_lower(last, c0, PAIR, on_vector=True)
+        mirrored = [(i0, min(2, last - i0)) for i0 in range(0, last, 2)]
+        for i0, n in mirrored:
             turn_t(last, i0, n)
-        store_lower(last, 0, BANK, on_vector=True)
-        store_lower(last, BANK, BANK, on_vector=True)
-        store_upper(last, 0, 4, on_vector=False)
-        store_upper(last, 4, 3, on_vector=True)
+        for turn, (i0, n) in enumerate(mirrored):
+            store_upper(last, i0, n, on_vector=(turn % 2 == 1))

from contextlib import ExitStack

import concourse.mybir as mybir
from concourse.masks import make_identity

N, D, H = 1024, 512, 1024
FLOPS = 2 * (2 * N * D * H) + 2 * N * N * H

F32 = mybir.dt.float32
BF16 = mybir.dt.bfloat16
I32 = mybir.dt.int32
U32 = mybir.dt.uint32
U8 = mybir.dt.uint8
FP8 = mybir.dt.float8_e4m3fn
FP8X4 = mybir.dt.float8_e4m3fn_x4
ACT = mybir.ActivationFunctionType
ALU = mybir.AluOpType

P = 128
PACK = 4
RUN = 8
BANK = 512
PAIR = 2 * P
CHUNKS = N // P
PASSES = H // (P * PACK)
SIDES = 2
SCORE_SCALE = -1.5 / 32.0


def tile_mtgnnantisymmetricgraphlearner_w8_kernel(
    tc, e1, e2_bytes, e2_scale, w1_words, w1_scales, w2_words, w2_scales, g1, g2, out
):
    nc = tc.nc
    with ExitStack() as ctx:
        keep = ctx.enter_context(tc.tile_pool(name="keep", bufs=1))
        work = ctx.enter_context(tc.tile_pool(name="work", bufs=3))
        results = ctx.enter_context(tc.tile_pool(name="results", bufs=5))
        tanh_pool = ctx.enter_context(tc.tile_pool(name="tanh", bufs=10))
        banks = ctx.enter_context(tc.psum_pool(name="banks", bufs=7))
        gain_bank = ctx.enter_context(tc.psum_pool(name="gain_bank", bufs=1))
        ctx.enter_context(tc.manual_schedule())

        ident = keep.tile([P, P], F32, name="ident")
        pick_rows = keep.tile([P, SIDES * PACK], BF16, name="pick_rows")
        gain_rows = keep.tile([P, PASSES * P], BF16, name="gain_rows")
        scale_cols = keep.tile([P, PACK], F32, name="scale_cols")
        scale_spread = keep.tile([P, 2 * D], F32, name="scale_spread")
        gain_spread = keep.tile([P, BANK], F32, name="gain_spread")
        m2_last = keep.tile([P, 2 * BANK], BF16, name="m2_last", align_bytes=64)
        gains = gain_bank.tile([P, PASSES * SIDES * PACK], F32, name="gains")

        w_raw = [keep.tile([P, H], U32, name="w_raw%d" % s) for s in range(SIDES)]
        ws_raw = [keep.tile([P, H], U8, name="ws_raw%d" % s) for s in range(SIDES)]
        w_codes = [[keep.tile([P, BANK], U32, name="w_codes%d%d" % (s, g), align_bytes=64) for g in range(PASSES)] for s in range(SIDES)]
        w_scale = [keep.tile([P, H], U8, name="w_scale%d" % s, align_bytes=64) for s in range(SIDES)]

        e_loads = [(0, 2), (2, 2), (4, 4)]
        e1_tiles = [keep.tile([P, n * D], BF16, name="e1_rows%d" % c0) for c0, n in e_loads]
        e2_tiles = [keep.tile([P, n * D], U8, name="e2_fp8_rows%d" % c0) for c0, n in e_loads]
        e_rows = [{}, {}]
        e2_fp8 = {}
        for (c0, n), e1_tile, e2_tile in zip(e_loads, e1_tiles, e2_tiles):
            for j in range(0, n, 2):
                e_rows[0][(c0 + j) // 2] = e1_tile[:, j * D : (j + 2) * D]
                e2_fp8[(c0 + j) // 2] = e2_tile[:, j * D : (j + 2) * D]

        m_codes = [[keep.tile([P, N], U32, name="m_codes%d%d" % (s, g), align_bytes=64) for g in range(PASSES)] for s in range(SIDES)]
        m_scale = [[keep.tile([P, N], U8, name="m_scale%d%d" % (s, g), align_bytes=64) for g in range(PASSES)] for s in range(SIDES)]

        e_turned, e_grouped, e_mx = {}, {}, {}
        proj, tanh_vals, m_bf16, m1_whole, neg_bf16, neg_mx = {}, {}, {}, {}, {}, {}
        score, t_vals, t_turned = {}, {}, {}

        def load_rows(dst, src, c0, n):
            nc.sync.dma_start(
                out=dst[:].rearrange("p (c k) -> p c k", k=D),
                in_=src[c0 * P : (c0 + n) * P, :].rearrange("(c p) k -> p c k", p=P),
            )

        def load_w_words(s, src):
            nc.sync.dma_start(out=w_raw[s][:].bitcast(I32), in_=src[0].rearrange("p n t -> p (n t)").bitcast(I32))

        def load_w_scales(s, src):
            for q in range(4):
                nc.sync.dma_start(
                    out=ws_raw[s][32 * q : 32 * q + 4, :].bitcast(I32),
                    in_=src[0, 4 * q : 4 * q + 4, :].bitcast(I32),
                )

        def order_w_scales(s):
            words = RUN // 4
            nc.vector.tensor_copy(
                out=w_scale[s][:].bitcast(I32).rearrange("p (g t b r) -> p g t b r", g=PASSES, t=PACK, r=words),
                in_=ws_raw[s][:].bitcast(I32).rearrange("p (g b t r) -> p g t b r", g=PASSES, t=PACK, r=words),
            )

        def order_w_codes(s, g):
            nc.vector.tensor_copy(
                out=w_codes[s][g][:].bitcast(I32).rearrange("p (t b r) -> p t b r", t=PACK, r=RUN),
                in_=w_raw[s][:, g * BANK : (g + 1) * BANK].bitcast(I32).rearrange("p (b t r) -> p t b r", t=PACK, r=RUN),
            )

        def scale_e2(pair):
            rows = work.tile([P, 2 * D], BF16, name="e2_rows")
            nc.vector.tensor_tensor(out=rows[:], in0=e2_fp8[pair].bitcast(FP8), in1=scale_spread[:], op=ALU.mult)
            e_rows[1][pair] = rows[:]

        def turn_e(pair, s):
            bank = banks.tile([P, BANK], F32, name="bank")
            twos = e_rows[s][pair].bitcast(F32)
            for j in range(2):
                for u in range(2):
                    col = (2 * j + u) * P
                    nc.tensor.transpose(bank[:, col : col + P], twos[:, j * 2 * P + u : (j + 1) * 2 * P : 2], ident[:])
            e_turned[pair, s] = bank

        def group_e(pair, s):
            if s == 0:
                e_grouped[pair] = work.tile([P, SIDES * PAIR * PACK], BF16, name="e_grouped", align_bytes=64)
            nc.scalar.copy(
                out=e_grouped[pair][:].bitcast(F32)[:, s * BANK : (s + 1) * BANK].rearrange("p (j n u) -> p j n u", n=P, u=2),
                in_=e_turned[pair, s][:].rearrange("p (j u n) -> p j n u", n=P, u=2),
            )

        def quantize_e(pair, first, sides):
            codes = keep.tile([P, sides * PAIR], U32, name="e_codes%d%d" % (pair, first), align_bytes=64)
            scale = keep.tile([P, sides * PAIR], U8, name="e_scale%d%d" % (pair, first), align_bytes=64)
            nc.vector.quantize_mx(
                out=codes[:].bitcast(FP8X4),
                scales=scale[:],
                in_=e_grouped[pair][:, first * PAIR * PACK : (first + sides) * PAIR * PACK],
            )
            for i in range(sides):
                e_mx[pair, first + i] = (codes[:, i * PAIR : (i + 1) * PAIR], scale[:, i * PAIR : (i + 1) * PAIR])

        def turn_and_group_e(pair):
            for s in range(SIDES):
                turn_e(pair, s)
            for s in range(SIDES):
                group_e(pair, s)

        def project(pair, s, g, j):
            codes, scale = e_mx[pair, s]
            bank = banks.tile([P, BANK], F32, name="bank")
            for t in range(PACK):
                nc.tensor.matmul_mx(
                    out=bank[:, t * P : (t + 1) * P],
                    lhsT=w_codes[s][g][:, t * P : (t + 1) * P].bitcast(FP8X4),
                    lhsT_scale=w_scale[s][:, g * BANK + t * P : g * BANK + (t + 1) * P],
                    rhs=codes[:, j * P : (j + 1) * P].bitcast(FP8X4),
                    rhs_scale=scale[:, j * P : (j + 1) * P],
                    start=True,
                    stop=True,
                )
            proj[pair, s, g, j] = bank

        def tanh_proj(pair, s, g, j):
            if j == 0:
                tanh_vals[pair, s, g] = tanh_pool.tile([P, 2 * BANK], F32, name="tanh_vals")
            nc.scalar.activation(
                out=tanh_vals[pair, s, g][:, j * BANK : (j + 1) * BANK].rearrange("p (n t) -> p n t", t=PACK),
                in_=proj[pair, s, g, j][:].rearrange("p (t n) -> p n t", t=PACK),
                func=ACT.Tanh,
            )

        def project_all(pair, s):
            for g in range(PASSES):
                for j in range(2):
                    project(pair, s, g, j)

        def tanh_all(pair, s):
            for g in range(PASSES):
                for j in range(2):
                    tanh_proj(pair, s, g, j)

        def project_side(pair, s):
            project_all(pair, s)
            tanh_all(pair, s)

        def m_tile(c, n, s, g):
            if s == 1 and g == PASSES - 1:
                m_bf16[c, s, g] = m2_last[:, 0 : n * BANK]
            elif s == 1:
                m2_first = work.tile([P, 2 * BANK], BF16, name="m2_first", align_bytes=64)
                m_bf16[c, s, g] = m2_first[:, 0 : n * BANK]
            elif g == 0:
                m1_whole[c] = work.tile([P, PASSES * 2 * BANK], BF16, name="m1_whole", align_bytes=64)
                for i in range(PASSES):
                    m_bf16[c, s, i] = m1_whole[c][:, i * n * BANK : (i + 1) * n * BANK]
            return m_bf16[c, s, g]

        def apply_gain(c, n, s, g, done):
            start = (c % 2) * BANK
            cols = (n - done) * BANK
            col = (SIDES * g + s) * PACK
            nc.vector.tensor_tensor(
                out=m_tile(c, n, s, g)[:, 0:cols].rearrange("p (n t) -> p n t", t=PACK),
                in0=tanh_vals[c // 2, s, g][:, start : start + cols].rearrange("p (n t) -> p n t", t=PACK),
                in1=gains[:, col : col + PACK].unsqueeze(1).to_broadcast([P, cols // PACK, PACK]),
                op=ALU.mult,
            )

        def apply_last_gain_on_gpsimd(c, n, taken):
            end = (c % 2 + n) * BANK
            cols = taken * BANK
            nc.gpsimd.tensor_tensor(
                out=m_tile(c, n, 1, PASSES - 1)[:, n * BANK - cols : n * BANK].rearrange("p (j x) -> p j x", j=taken),
                in0=tanh_vals[c // 2, 1, PASSES - 1][:, end - cols : end].rearrange("p (j x) -> p j x", j=taken),
                in1=gain_spread[:].unsqueeze(1).to_broadcast([P, taken, BANK]),
                op=ALU.mult,
            )

        def quantize_m(c, n, s, g):
            nodes = slice(c * P, (c + n) * P)
            nc.vector.quantize_mx(
                out=m_codes[s][g][:, nodes].bitcast(FP8X4), scales=m_scale[s][g][:, nodes], in_=m_bf16[c, s, g]
            )

        def negate_m1(c, n):
            width = PASSES * n * BANK
            neg = work.tile([P, PASSES * 2 * BANK], BF16, name="neg_bf16", align_bytes=64)
            nc.vector.tensor_scalar(out=neg[:, 0:width], in0=m1_whole[c][:, 0:width], scalar1=-1.0, scalar2=None, op0=ALU.mult)
            neg_bf16[c] = neg

        def quantize_neg(c, n):
            width = PASSES * n * P
            codes = work.tile([P, PASSES * PAIR], U32, name="neg_codes", align_bytes=64)
            scale = work.tile([P, PASSES * PAIR], U8, name="neg_scale", align_bytes=64)
            nc.vector.quantize_mx(out=codes[:, 0:width].bitcast(FP8X4), scales=scale[:, 0:width], in_=neg_bf16[c][:, 0 : width * PACK])
            for j in range(n):
                for g in range(PASSES):
                    cols = slice((g * n + j) * P, (g * n + j + 1) * P)
                    neg_mx[c + j, g] = (codes[:, cols], scale[:, cols])

        def gain_products(c, n):
            apply_last_gain_on_gpsimd(c, n, n)
            apply_gain(c, n, 0, 0, 0)
            apply_gain(c, n, 0, 1, 0)
            apply_gain(c, n, 1, 0, 0)

        def quantize_all_but_last(c, n):
            negate_m1(c, n)
            quantize_m(c, n, 0, 0)
            quantize_m(c, n, 0, 1)
            quantize_neg(c, n)
            quantize_m(c, n, 1, 0)

        def quantize_last(c, n):
            quantize_m(c, n, 1, PASSES - 1)

        def spans(c):
            width = (c + 1) * P
            return [(c0, min(BANK, width - c0)) for c0 in range(0, width, BANK)]

        def score_span(c, c0, width):
            bank = banks.tile([P, BANK], F32, name="bank")
            nodes = slice(c * P, (c + 1) * P)
            steps = [neg_mx[c, g] + (1, g) for g in range(PASSES)]
            steps = steps + [(m_codes[1][g][:, nodes], m_scale[1][g][:, nodes], 0, g) for g in range(PASSES)]
            groups = [(0, PAIR), (PAIR, P)] if width == PAIR + P else [(0, width)]
            for off, n in groups:
                cols = slice(c0 + off, c0 + off + n)
                for i, (lhs, lhs_scale, s, g) in enumerate(steps):
                    nc.tensor.matmul_mx(
                        out=bank[:, off : off + n],
                        lhsT=lhs.bitcast(FP8X4),
                        lhsT_scale=lhs_scale,
                        rhs=m_codes[s][g][:, cols].bitcast(FP8X4),
                        rhs_scale=m_scale[s][g][:, cols],
                        start=(i == 0),
                        stop=(i == len(steps) - 1),
                    )
            score[c, c0] = bank

        def tanh_span(c, c0, width):
            if c0 == 0:
                t_vals[c] = results.tile([P, N], F32, name="t_vals")
            nc.scalar.activation(out=t_vals[c][:, c0 : c0 + width], in_=score[c, c0][:, 0:width], func=ACT.Tanh, scale=SCORE_SCALE)

        def score_row(c):
            for c0, width in spans(c):
                score_span(c, c0, width)
            for c0, width in spans(c):
                tanh_span(c, c0, width)

        def store_lower(c, c0, width, on_vector):
            res = results.tile([P, N], F32, name="lower")
            src = t_vals[c][:, c0 : c0 + width]
            if on_vector:
                nc.vector.tensor_scalar(out=res[:, 0:width], in0=src, scalar1=0.0, scalar2=None, op0=ALU.max)
            else:
                nc.scalar.activation(out=res[:, 0:width], in_=src, func=ACT.Relu)
            nc.sync.dma_start(out=out[c * P : (c + 1) * P, c0 : c0 + width], in_=res[:, 0:width])

        def store_lower_row(c, on_vector):
            store_lower(c, 0, (c + 1) * P, on_vector)

        def relu_of_negative(dst, src, on_vector):
            if on_vector:
                nc.vector.tensor_scalar(out=dst, in0=src, scalar1=-1.0, scalar2=0.0, op0=ALU.mult, op1=ALU.max)
            else:
                nc.scalar.activation(out=dst, in_=src, func=ACT.Relu, scale=-1.0)

        def turn_t(c, i0, n):
            bank = banks.tile([P, BANK], F32, name="bank")
            for i in range(n):
                nc.tensor.transpose(bank[:, i * P : (i + 1) * P], t_vals[c][:, (i0 + i) * P : (i0 + i + 1) * P], ident[:])
            t_turned[c, i0] = bank

        def store_upper(c, i0, n, on_vector):
            res = results.tile([P, BANK], F32, name="upper")
            relu_of_negative(res[:, 0 : n * P], t_turned[c, i0][:, 0 : n * P], on_vector)
            nc.sync.dma_start(
                out=out[i0 * P : (i0 + n) * P, c * P : (c + 1) * P].rearrange("(i p) n -> p i n", p=P),
                in_=res[:, 0 : n * P].rearrange("p (i n) -> p i n", n=P),
            )

        def mirror_row(c):
            blocks = [(i0, min(BANK // P, c - i0)) for i0 in range(0, c, BANK // P)]
            for i0, n in blocks:
                turn_t(c, i0, n)
            for i0, n in blocks:
                store_upper(c, i0, n, on_vector=False)

        def mirror_pair(pair):
            c = 2 * pair
            turned = []
            for i0 in range(0, c, 2):
                bank = banks.tile([P, BANK], F32, name="bank")
                for i in range(2):
                    for j in range(2):
                        col = (2 * i + j) * P
                        nc.tensor.transpose(bank[:, col : col + P], t_vals[c + j][:, (i0 + i) * P : (i0 + i + 1) * P], ident[:])
                turned.append((i0, bank))
            turn_t(c + 1, c, 1)
            for i0, bank in turned:
                res = results.tile([P, BANK], F32, name="upper")
                relu_of_negative(res[:], bank[:], on_vector=False)
                nc.sync.dma_start(
                    out=out[i0 * P : (i0 + 2) * P, c * P : (c + 2) * P].rearrange("(i p) n -> p i n", p=P),
                    in_=res[:].rearrange("p (i n) -> p i n", n=PAIR),
                )
            store_upper(c + 1, c, 1, on_vector=False)

        make_identity(nc, ident[:])
        nc.vector.memset(ws_raw[0][:].bitcast(I32), 0)
        nc.vector.memset(gain_rows[:], 0.0)
        nc.vector.memset(ws_raw[1][:].bitcast(I32), 0)
        for s, gain in enumerate((g1, g2)):
            nc.gpsimd.dma_start(
                out=gain_rows[s * PACK : (s + 1) * PACK, :].rearrange("t (q r) -> t q r", r=RUN),
                in_=gain.rearrange("(q t r) -> t q r", t=PACK, r=RUN),
            )
        nc.vector.tensor_copy(out=pick_rows[:], in_=ident[:, 0 : SIDES * PACK])

        nc.sync.dma_start(out=scale_cols[:], in_=e2_scale.rearrange("o (n t) -> n (o t)", t=PACK))
        load_rows(e1_tiles[0], e1, *e_loads[0])
        load_rows(e1_tiles[1], e1, *e_loads[1])
        load_w_words(0, w1_words)
        load_w_scales(0, w1_scales)
        load_rows(e2_tiles[0], e2_bytes, *e_loads[0])
        load_rows(e2_tiles[1], e2_bytes, *e_loads[1])
        load_w_words(1, w2_words)
        load_w_scales(1, w2_scales)
        load_rows(e2_tiles[2], e2_bytes, *e_loads[2])
        load_rows(e1_tiles[2], e1, *e_loads[2])

        spread_bank = banks.tile([P, BANK], F32, name="bank")
        for t in range(PACK):
            nc.tensor.transpose(spread_bank[:, t * P : (t + 1) * P], scale_cols[:, t : t + 1].to_broadcast([P, P]), ident[:])
        nc.scalar.activation(
            out=scale_spread[:].rearrange("p (j n t) -> p j n t", j=2, t=PACK),
            in_=spread_bank[:].rearrange("p (t n) -> p n t", t=PACK).unsqueeze(1).to_broadcast([P, 2, P, PACK]),
            func=ACT.Copy,
        )

        turn_e(0, 0)
        group_e(0, 0)
        turn_e(1, 0)
        group_e(1, 0)
        order_w_codes(0, 0)
        quantize_e(0, 0, 1)
        order_w_scales(0)
        order_w_codes(0, 1)
        scale_e2(0)
        quantize_e(1, 0, 1)
        scale_e2(1)
        project_all(0, 0)
        for g in range(PASSES):
            nc.tensor.matmul(
                gains[:, g * SIDES * PACK : (g + 1) * SIDES * PACK],
                lhsT=gain_rows[:, g * P : (g + 1) * P],
                rhs=pick_rows[:],
                start=True,
                stop=True,
            )
        last_gain = banks.tile([P, BANK], F32, name="bank")
        nc.tensor.matmul(
            last_gain[:, 0:PACK], lhsT=gain_rows[:, (PASSES - 1) * P : PASSES * P], rhs=pick_rows[:, PACK : 2 * PACK], start=True, stop=True
        )
        turn_e(0, 1)
        tanh_all(0, 0)
        nc.scalar.activation(
            out=gain_spread[:].rearrange("p (n t) -> p n t", t=PACK),
            in_=last_gain[:, 0:PACK].unsqueeze(1).to_broadcast([P, P, PACK]),
            func=ACT.Copy,
        )
        group_e(0, 1)
        project_side(1, 0)
        turn_e(1, 1)
        group_e(1, 1)

        order_w_codes(1, 0)
        order_w_codes(1, 1)
        order_w_scales(1)
        apply_gain(0, 2, 0, 0, 0)
        quantize_e(0, 1, 1)
        apply_gain(0, 2, 0, 1, 0)
        scale_e2(2)
        negate_m1(0, 2)
        quantize_m(0, 2, 0, 0)
        quantize_m(0, 2, 0, 1)
        quantize_e(1, 1, 1)
        project_side(0, 1)
        turn_and_group_e(2)
        scale_e2(3)
        apply_last_gain_on_gpsimd(0, 2, 1)
        apply_gain(0, 2, 1, 0, 0)
        apply_gain(0, 2, 1, 1, 1)
        quantize_neg(0, 2)
        quantize_e(2, 0, SIDES)
        quantize_m(0, 2, 1, 0)
        quantize_last(0, 2)
        project_side(1, 1)
        turn_and_group_e(3)
        project_side(2, 0)
        score_row(0)
        score_row(1)

        gain_products(2, 2)
        quantize_e(3, 0, SIDES)
        quantize_all_but_last(2, 2)
        quantize_last(2, 2)
        project_side(2, 1)
        mirror_pair(0)
        store_lower_row(0, on_vector=False)
        store_lower_row(1, on_vector=False)
        project_side(3, 0)
        score_row(2)
        score_row(3)
        project_side(3, 1)

        gain_products(4, 1)
        quantize_all_but_last(4, 1)
        quantize_last(4, 1)
        mirror_pair(1)
        store_lower_row(2, on_vector=False)

        gain_products(5, 1)
        quantize_all_but_last(5, 1)
        store_lower_row(3, on_vector=True)
        quantize_last(5, 1)
        score_row(4)
        score_row(5)
        mirror_row(4)

        gain_products(6, 1)
        quantize_all_but_last(6, 1)
        store_lower_row(4, on_vector=True)
        quantize_last(6, 1)
        store_lower_row(5, on_vector=False)
        mirror_row(5)
        score_row(6)

        last = CHUNKS - 1
        gain_products(last, 1)
        quantize_all_but_last(last, 1)
        quantize_last(last, 1)
        store_lower_row(last - 1, on_vector=True)
        mirror_row(last - 1)

        quarters = range(0, N, PAIR)
        for c0 in quarters:
            score_span(last, c0, PAIR)
        for c0 in quarters:
            tanh_span(last, c0, PAIR)
        for c0 in quarters:
            store_lower(last, c0, PAIR, on_vector=True)
        mirrored = [(i0, min(2, last - i0)) for i0 in range(0, last, 2)]
        for i0, n in mirrored:
            turn_t(last, i0, n)
        for turn, (i0, n) in enumerate(mirrored):
            store_upper(last, i0, n, on_vector=(turn % 2 == 1))
